import numpy as np, ml_dtypes
CORES = [3,7,11,15,131,135,139,143]
N = 8
import mx_ref
BF = ml_dtypes.bfloat16
def cut(t, i, w=512):
    return t[:, w * i:w * i + w]
def tile(rs):
    return np.stack(rs, axis=2).reshape(128, -1).astype(BF)
def pick(q, e):
    c = np.concatenate([q[0].reshape(128, -1, 4), np.zeros((128, 1, 4), np.uint8)], axis=1); s = np.concatenate([q[1], np.ones((16, 1), np.uint8)], axis=1)
    return (np.ascontiguousarray(c[:, e].reshape(128, -1)), np.ascontiguousarray(s[:, e]))
def join(*qs):
    return (np.concatenate([q[0] for q in qs], axis=1), np.concatenate([q[1] for q in qs], axis=1))
def put(q, e, v):
    c, s = q[0].reshape(128, -1, 4).copy(), q[1].copy(); c[:, e] = v[0].reshape(128, -1, 4); s[:, e] = v[1]
    return (c.reshape(128, -1), s)
def pk(c, s):
    return (np.ascontiguousarray(c), mx_ref.live(s))
def emit(q):
    return q[0], q[1]
def f(rng, *shape):
    return mx_ref.flush((rng.standard_normal(shape, dtype=np.float32) * np.exp2(rng.integers(-2, 3, shape[:-1] + (1,)))).astype(BF))
def wide(rng, *shape, cols=0):
    v = rng.standard_normal(shape, dtype=np.float32) * np.exp2(rng.integers(-12, 13, shape)).astype(np.float32)
    if cols: v *= np.repeat(np.exp2(rng.integers(-cols, cols + 1, shape[:-2] + (1, shape[-1] // 4))) * (rng.random(shape[:-2] + (1, shape[-1] // 4)) > 0.0625), 4, axis=-1).astype(np.float32)
    return mx_ref.flush(v.astype(BF))
T, G, CS, R = 64, 64, 16, 3
def game(x, qx, w, u):
    wq = [[mx_ref.quantize(np.ascontiguousarray(cut(w[r], i))) for i in range(4)] for r in range(N)]
    uq = [mx_ref.quantize(np.ascontiguousarray(u[r])) for r in range(N)]
    wait = join(*[mx_ref.quantize(np.ascontiguousarray(qx[m])) for m in range(N)])
    s = [mx_ref.quantize(np.ascontiguousarray(x[r])) for r in range(N)]
    num = [r * T + np.arange(T) for r in range(N)]
    log, said, made, head = [[] for r in range(N)], [[] for r in range(N)], [], 0
    for t in range(R):
        for r in range(N):
            a = tile([np.maximum(mx_ref.matmul(wq[r][i], s[r]), np.float32(0)) * np.float32(0.0625) for i in range(4)])
            made.append(a)
            s[r] = mx_ref.quantize(a)
            h = mx_ref.matmul(uq[r], s[r])[:2] + np.float32(0)
            stop = np.flatnonzero(h[0] > h[1])[:CS]
            if stop.size == 0: continue
            log[r].append(pick(s[r], stop))
            said[r].extend(num[r][stop].tolist())
            g = head + np.arange(stop.size)
            s[r] = put(s[r], stop, pick(wait, G * (g % N) + g // N))
            num[r][stop] = N * T + g
            head += stop.size
    return log, said, s, num, made
def fit(d, top=2.0 ** 30):
    try:
        with np.errstate(all="ignore"):
            a = np.abs(np.stack(game(d["x"], d["qx"], d["w"], d["u"])[4]).astype(np.float32))
    except Exception: return False
    return bool(np.isfinite(a).all() and ((a == 0) | (a >= 2.0 ** -30) & (a <= top)).all())
def first(make, top=2.0 ** 30):
    for i in range(5):
        d = make()
        if fit(d, top): break
    return d
def plain(rng):
    w = np.rint(rng.standard_normal((N, 128, 2048), dtype=np.float32) * 8) * 0.125 * np.exp2(rng.integers(-1, 2, (N, 128, 1))) + 0.0
    u = np.zeros((N, 128, 512), np.float32)
    u[:, :, :8] = rng.standard_normal((N, 128, 8))
    u[:, :, 4:8] += 0.15 * rng.random((N, 1, 1))
    u *= np.exp2(rng.integers(-1, 2, (N, 128, 1)))
    return {"x": np.array(f(rng, N, 128, 4 * T)), "qx": np.array(f(rng, N, 128, 4 * G)), "w": w.astype(BF), "u": np.array(mx_ref.flush(u.astype(BF))), "v": np.array(f(rng, N, 128, 512))}
def channel(w, alone=False):
    a = w.astype(np.float32).reshape(N, 128, 4, 128, 4)
    if alone: a[:, :8] = 0
    a[:, :, :, :8, :] = 0
    for i in range(4):
        for j in range(8): a[:, j, i, j, i] = 16
    return a.reshape(N, 128, 2048).astype(BF)
def flags(d, live, wait):
    d["x"][:, :8] = np.repeat(np.where(live, 4.0, 0.0), 4, axis=1)[:, None, :].astype(BF)
    d["qx"][:, :8] = np.repeat(np.where(wait.reshape(G, N).T, 4.0, 0.0), 4, axis=1)[:, None, :].astype(BF)
def signed(t, a, b):
    o = np.abs(t.astype(np.float32))
    o[:, :4] *= a
    o[:, 4:8] *= b
    return o.astype(BF)
def setup_inputs(rng):
    return first(lambda: plain(rng), 2.0 ** 8)
def setup_inputs_many(rng):
    def make():
        d = plain(rng)
        d["w"] = channel(d["w"])
        pair = rng.integers(0, 2, N * G // 2)
        flags(d, np.stack([rng.permutation(T) < 3 * T // 4 for r in range(N)]), np.stack([pair, 1 - pair], axis=1).reshape(-1) == 1)
        for r in range(N):
            a = np.zeros((128, 512), np.float32)
            a[:8, :4] = 1
            a[8:, 4:8] = np.abs(rng.standard_normal((120, 4))) * 2.0 ** -8
            d["u"][r] = mx_ref.flush(a.astype(BF))
        return d
    return first(make)
def setup_inputs_none(rng):
    def make():
        d = plain(rng)
        a, b = rng.permutation(N)[:2]
        d["u"][a] = signed(d["u"][a], -1, 1)
        d["u"][b] = signed(d["u"][b], 1, -1)
        return d
    return first(make)
def setup_inputs_ties(rng):
    def make():
        d = plain(rng)
        d["w"] = channel(d["w"])
        flags(d, np.stack([rng.permutation(T) < T // 3 for r in range(N)]), rng.random(N * G) < 0.3)
        d["u"][:, :, 4:8] = d["u"][:, :, :4]
        d["u"][:, :8, :4] = 1
        d["u"][:, :8, 4:8] = 0
        a, c = rng.permutation(N)[:2]
        d["u"][a, :, 4:8] = d["u"][a, :, :4]
        d["u"][c] = 0
        d["u"][c, :7, :8] = 1
        d["u"][c, 7, :4] = 2.0 ** -8
        d["u"][c, 7, 4:8] = 2.0 ** -9
        return d
    return first(make)
def setup_inputs_zero(rng):
    def make():
        d = plain(rng)
        d["w"] = channel(d["w"], alone=True)
        live = np.stack([rng.permutation(np.repeat([0, 1, 2], [T - 2 * (T // 8), T // 8, T // 8])) for r in range(N)])
        for k, e in (("x", live), ("qx", rng.choice(3, (N, G), p=[0.75, 0.125, 0.125]))):
            m = np.repeat(e, 4, axis=1)[:, None, :]
            c = np.where(m == 0, d[k].astype(np.float32), np.float32(0))
            c[:, :8] = np.where(m == 2, np.float32(-4), c[:, :8])
            d[k] = c.astype(BF)
        for r in rng.permutation(N)[:N // 2]: d["u"][r] = signed(d["u"][r], 1, -1)
        return d
    return first(make)
def setup_inputs_spread(rng):
    return first(lambda: {**plain(rng), "x": wide(rng, N, 128, 4 * T, cols=6), "qx": wide(rng, N, 128, 4 * G, cols=6)})
def check_inputs(d):
    b = []
    for k in ("x", "qx", "w", "u", "v"):
        a = np.abs(d[k].astype(np.float32))
        if not (np.isfinite(a).all() and ((a == 0) | (a >= 2.0 ** -30) & (a <= 2.0 ** 30)).all()): b.append("a value of " + k)
    if (d["u"][:, :, 8:].astype(np.float32) != 0).any(): b.append("u has numbers behind its first two columns")
    if not b and not fit(d): b.append("a number that a layer makes")
    return b
def reference(x, qx, w, u, v):
    log, said, s, num, made = game(x, qx, w, u)
    M = R * CS + T
    oc, osc = np.zeros((N, 128, 4 * M), np.uint8), np.zeros((N, 16, M), np.uint8)
    sid, y = np.full((N, 1, M), -1, np.float32), np.zeros((N, 128, T), np.float32)
    for r in range(N):
        n = len(said[r])
        oc[r], osc[r] = emit(pick(join(*log[r], s[r]), np.concatenate([np.arange(n), np.full(R * CS - n, -1), n + np.arange(T)])))
        sid[r, 0, :n] = said[r]
        sid[r, 0, R * CS:] = num[r]
        y[r] = mx_ref.matmul(mx_ref.quantize(np.ascontiguousarray(v[r])), s[r])
    return {"oc": oc, "osc": osc, "sid": sid, "y": y}

@@ -1,0 +1,333 @@
+from concourse.bass import DstId, RemoteDMATransfer
+from concourse.mybir import dt, AluOpType, AxisListType, ActivationFunctionType
+
+NR, PL, CS, RD = 8, 64, 16, 3
+USED = RD * CS
+PICK, SELF, LAND, ZW = 128, 140, 144, 160
+
+SCRATCH = {
+    "wt": ("sbuf", [128, 2048], "bfloat16"), "xt": ("sbuf", [128, 512], "bfloat16"),
+    "qt": ("sbuf", [128, 512], "bfloat16"), "ut": ("sbuf", [128, 512], "bfloat16"), "vt": ("sbuf", [128, 512], "bfloat16"),
+    "fl": ("sbuf", [128, 3000], "float32"), "il": ("sbuf", [128, 256], "int32"), "ol": ("sbuf", [128, 128], "uint16"),
+    "sidc": ("sbuf", [128, 80], "float32"), "sidl": ("sbuf", [128, 48], "float32"), "ys": ("sbuf", [128, 64], "float32"),
+    "ha": ("psum", [128, 512], "float32"), "hb": ("psum", [128, 512], "float32"), "py": ("psum", [128, 512], "float32"),
+}
+for _n, _w in (("wc", 512), ("uq", 128), ("ua", 128), ("ub", 128), ("vq", 128), ("wq", 256), ("cc", 80), ("lg", 48),
+               ("x0", 128), ("x1", 128), ("x2", 128), ("x3", 128), ("z0", ZW), ("z1", ZW), ("z2", ZW)):
+    SCRATCH[_n] = ("sbuf", [128, _w], "float8_e4m3fn_x4")
+    SCRATCH[_n + "s"] = ("sbuf", [128, _w], "uint8")
+for _t in range(RD):
+    SCRATCH["at%d" % _t] = ("sbuf", [128, 512], "bfloat16")
+    SCRATCH["sat%d" % _t] = ("sbuf", [128, 72], "float32")
+    SCRATCH["cnt%d" % _t] = ("sbuf", [128, 8], "float32")
+for _t in range(RD + 1):
+    SCRATCH["num%d" % _t] = ("sbuf", [128, 72], "float32")
+    SCRATCH["pz%d" % _t] = ("psum", [128, 512], "float32")
+SEMAPHORES = ["vs", "ss", "ts", "gs", "lqx", "lu", "lx", "lv", "lw0", "lw1", "lw2", "lw3", "pad", "st", "pre", "loc"]
+SEMAPHORES += [k + str(t) for k in ("ac", "ak", "ap") for t in range(RD)]
+
+
+def rank_program(g, core, T, topo):
+    rank = T.rank_of(core)
+    if rank is None:
+        return
+    A, AF = AluOpType, ActivationFunctionType
+    v, s, te, sy = g.vector, g.scalar, g.tensor, g.sync
+    u8, u32 = dt.uint8, dt.uint32
+    chips = []
+    for c in T.cores:
+        if not any(c in topo.cores_of(q[0]) for q in chips):
+            chips.append([d for d in T.cores if d in topo.cores_of(c)])
+    nch = len(chips)
+    me = [i for i in range(nch) if core in chips[i]][0]
+    lane = chips[me].index(core)
+    mate = chips[me][1 - lane]
+    peers = [chips[(me + 1 + e) % nch][lane] for e in range(nch - 1)]
+    far = [c for c in T.cores if c not in chips[me]]
+    eoff = topo.engines(core, far[0])
+    eon = [e for e in topo.engines(core, mate) if e not in eoff]
+    ncnt = (NR - 2) * len(eoff) + len(eon)
+
+    def bits(es):
+        return sum(1 << e for e in es)
+
+    def did(d):
+        rid, pid = topo.addr(d, core)
+        return DstId(rid=rid, pnc=pid)
+
+    Q = {"v": v, "s": s, "t": te, "g": g, "y": sy}
+    own = {"v": "vs", "s": "ss", "t": "ts", "g": "gs"}
+    done = {"vs": 0, "ss": 0, "ts": 0, "gs": 0}
+    dmas = {}
+    seen = {q: {} for q in Q}
+
+    def need(q, deps):
+        top = {}
+        for n, c in deps:
+            top[n] = max(top.get(n, 0), c)
+        for n, c in top.items():
+            if seen[q].get(n, 0) < c:
+                Q[q].wait_ge(T.sem[n], c)
+                seen[q][n] = c
+
+    def run(q, deps, call, *a, **k):
+        need(q, deps)
+        n = own[q]
+        call(*a, **k).then_inc(T.sem[n], 1)
+        done[n] += 1
+        return (n, done[n])
+
+    def V(deps, call, *a, **k):
+        return run("v", deps, call, *a, **k)
+
+    def S(deps, call, *a, **k):
+        return run("s", deps, call, *a, **k)
+
+    def dma(q, deps, sem, out, in_):
+        need(q, deps)
+        Q[q].dma_start(out, in_).then_inc(T.sem[sem], 16)
+        dmas[sem] = dmas.get(sem, 0) + 16
+        return (sem, dmas[sem])
+
+    at = {"fl": 0, "il": 0, "ol": 0}
+
+    def take(buf, n):
+        a = at[buf]
+        at[buf] = a + n + (n % 2 if buf == "ol" else 0)
+        return T[buf][:, a:a + n]
+
+    def F(n):
+        return take("fl", n)
+
+    def I(n):
+        return take("il", n)
+
+    def O(n):
+        return take("ol", n)
+
+    tqx = dma("y", [], "lqx", T.qt[:, 0:4 * USED], T.qx[:, 0:4 * USED])
+    tx = dma("s", [], "lx", T.xt[:, 0:256], T.x[:, :])
+    tu = dma("y", [], "lu", T.ut[:, 0:8], T.u[:, 0:8])
+    tw = [dma("ys"[i % 2], [], "lw%d" % i, T.wt[:, 512 * i:512 * i + 512], T.w[:, 512 * i:512 * i + 512]) for i in range(4)]
+    tv = dma("s", [], "lv", T.vt[:, :], T.v[:, :])
+
+    def iota(out, pattern, base, cm, fl):
+        if fl:
+            return run("g", [], g.iota, out, pattern, base, cm, allow_small_or_imprecise_dtypes=True)
+        return run("g", [], g.iota, out, pattern, base, cm)
+
+    a0 = at["fl"]
+    neg, rs0, jw0 = F(7), F(64), F(4)
+    ip, ip2, jp = I(1), I(1), I(64)
+    t_ip = iota(ip, [[0, 1]], 0, 1, False)
+    t_ip2 = iota(ip2, [[0, 1]], 4 * (me + 1), 1, False)
+    ngs = []
+    if rank < NR - 1:
+        ngs.append(iota(T.fl[:, a0:a0 + 7 - rank], [[1, 7 - rank]], -7, 0, True))
+    if rank > 0:
+        ngs.append(iota(T.fl[:, a0 + 7 - rank:a0 + 7], [[1, rank]], 1 - rank, 0, True))
+    t_jp = iota(jp, [[1, 64]], 0, -1, False)
+    t_rs = iota(rs0, [[0, 4], [1, 16]], 0, 0, True)
+    t_jw0 = iota(jw0, [[16, 4]], 0, 0, True)
+    t_num = [iota(T.num0[:, 0:64], [[1, 64]], PL * rank, 0, True)]
+
+    t_qz = V([], v.memset, T.qt[:, 4 * USED:512], 0.0)
+    t_uz = V([], v.memset, T.ut[:, 8:512], 0.0)
+    t_xz = V([], v.memset, T.xt[:, 256:512], 0.0)
+    O(16)
+    V([], v.memset, T.ol[:, 0:8], 0)
+    t_lo = V([], v.memset, T.ol[:, 8:16], 1)
+    c16 = F(64)
+    t_c16 = V([], v.memset, c16, 16.0)
+    t_a0 = V([], v.memset, T.at0[:, 256:512], 0.0)
+    V([], v.memset, T.sat0[:, 0:1], 0.0)
+    hd = F(1)
+    t_hd = V([], v.memset, hd, 0.0)
+    S([t_xz], s.activation, T.at1[:, 256:512], T.xt[:, 256:512], AF.Copy)
+    S([], s.activation, T.at2[:, 256:512], T.xt[:, 256:512], AF.Copy)
+    for k in range(1, RD):
+        S([t_hd], s.activation, T["sat%d" % k][:, 0:1], hd, AF.Copy)
+    for k in range(RD):
+        S([t_c16], s.activation, T["num%d" % k][:, 64:72], T.fl[:, at["fl"] - 65:at["fl"] - 57], AF.Copy, scale=-0.0625)
+    t_fill = S([], s.activation, T.sidc[:, 48:80], T.fl[:, at["fl"] - 65:at["fl"] - 33], AF.Copy, scale=-0.0625)
+
+    ik, kcol, ic, dcol, mask7, sm = I(1), F(1), I(1), F(1), F(7), F(1)
+    ih, isl, hc0a, hc0 = I(1), I(1), F(1), F(1)
+    i16, m16, rst, jd = I(64), F(64), F(64), F(4)
+    jwa = at["fl"]
+    jw = F(4)
+    jq = T.fl[:, jwa:jwa + 3]
+    c_ik = V([t_ip], v.tensor_scalar, ik, ip, 15, None, A.bitwise_and)
+    c_ic = V([t_ip2], v.tensor_scalar, ic, ip2, 2, 3, A.logical_shift_right, A.bitwise_and)
+    c_ih = V([t_ip], v.tensor_scalar, ih, ip, 1, 1, A.logical_shift_right, A.bitwise_and)
+    c_is = V([t_ip], v.tensor_scalar, isl, ip, 1, None, A.bitwise_and)
+    c_i16 = V([t_jp], v.tensor_scalar, i16, jp, 15, None, A.bitwise_and)
+    c_k = V([c_ik], v.tensor_copy, kcol, ik)
+    c_d = V([c_ic], v.tensor_scalar, dcol, ic, 2.0, float(lane), A.mult, A.add)
+    c_ha = V([c_ih], v.tensor_scalar, hc0a, ih, 128.0 - 0.125, (3.5 - 2 * me) / 8.0, A.mult, A.add)
+    c_m16 = V([c_i16], v.tensor_scalar, m16, i16, 0.0, None, A.is_equal)
+    c_rs = V([t_rs], v.tensor_scalar, rst, rs0, 1.0, None, A.min)
+    c_jw = V([t_jw0, c_k], v.tensor_scalar, jw, jw0, kcol, None, A.add)
+    c_m7 = V(ngs + [c_d], v.tensor_scalar, mask7, neg, dcol, 0.0, A.add, A.is_gt)
+    c_sm = V([c_d], v.tensor_scalar, sm, dcol, float(rank), 0.125, A.is_gt, A.mult)
+    c_hc = V([c_ha, c_is], v.tensor_tensor, hc0, hc0a, isl, A.add)
+    c_jd = V([c_jw], v.tensor_scalar, jd, jw, -1.0, float(SELF), A.mult, A.add)
+
+    wb = 128 * lane
+    t_wq = V([tqx, t_qz], v.quantize_mx, T.wq[:, wb:wb + 128], T.wqs[:, wb:wb + 128], T.qt[:, :])
+    need("g", [t_wq])
+    rid, pid = topo.addr(mate, core)
+    g.remote_dma(T.wq[:, wb:wb + USED].bitcast(u8), T.wq[:, wb:wb + USED].bitcast(u8), T.sem.pre, T.sem.loc, pid, rid, topo.mask(core, mate))
+    g.remote_dma(T.wqs[:, wb:wb + USED], T.wqs[:, wb:wb + USED], T.sem.pre, T.sem.loc, pid, rid, topo.mask(core, mate))
+    npre = 2 * len(topo.engines(core, mate))
+    local = npre
+
+    t_uq = V([tu, t_uz], v.quantize_mx, T.uq[:, :], T.uqs[:, :], T.ut[:, :])
+    t_ub = [V([t_uq, t_lo], v.tensor_copy, T.ub[:, :].bitcast(u32), T.uq[:, :].bitcast(u32).indirect(T.ol[:, 8:16])),
+            S([t_uq, t_lo], s.activation, T.ubs[:, :], T.uqs[:, :].indirect(T.ol[:, 8:16]), AF.Copy)]
+    t_ua = [V([], v.tensor_copy, T.ua[:, :].bitcast(u32), T.uq[:, :].bitcast(u32).indirect(T.ol[:, 0:8])),
+            S([], s.activation, T.uas[:, :], T.uqs[:, :].indirect(T.ol[:, 0:8]), AF.Copy)]
+    t_X = [V([tx, t_xz], v.quantize_mx, T.x0[:, :], T.x0s[:, :], T.xt[:, :])]
+    t_w = [V([tw[i]], v.quantize_mx, T.wc[:, 128 * i:128 * i + 128], T.wcs[:, 128 * i:128 * i + 128], T.wt[:, 512 * i:512 * i + 512])
+           for i in range(4)]
+    for n in ("x1", "x2", "x3"):
+        dma("y", t_X, "pad", T[n][:, 64:128].bitcast(u8), T.x0[:, 64:128].bitcast(u8))
+        dma("y", t_X, "pad", T[n + "s"][:, 64:128], T.x0s[:, 64:128])
+    dma("y", t_X, "pad", T.cc[:, 48:80].bitcast(u8), T.x0[:, 64:96].bitcast(u8))
+    t_pad = dma("y", t_X, "pad", T.ccs[:, 48:80], T.x0s[:, 64:96])
+
+    hc, t_hc = hc0, c_hc
+    counts, t_lcs, t_lis = [], [], []
+    for t in range(RD):
+        Xc, Xs = T["x%d" % t], T["x%ds" % t]
+        Zc, Zs = T["z%d" % t], T["z%ds" % t]
+        Nc, Ns = T["x%d" % (t + 1)], T["x%ds" % (t + 1)]
+        At, sat, land = T["at%d" % t], T["sat%d" % t], T["cnt%d" % t]
+        num, numn = T["num%d" % t], T["num%d" % (t + 1)]
+        t_mm = [run("t", t_X + [t_w[i]] + ([t_pad] if t else []), te.matmul_mx, T["pz%d" % i][:, 0:128], T.wc[:, 128 * i:128 * i + 128],
+                    T.wcs[:, 128 * i:128 * i + 128], Xc[:, 0:128], Xs[:, 0:128], True, True) for i in range(4)]
+        t_r = []
+        for i in range(4):
+            o, z = At[:, i:256:4], T["pz%d" % i][:, 0:64]
+            if i % 2:
+                t_r.append(V([t_mm[i]], v.tensor_scalar, o, z, 0.0, 0.0625, A.max, A.mult))
+            else:
+                t_r.append(S([t_mm[i]], s.activation, o, z, AF.Relu, scale=0.0625))
+        t_z = V(t_r + [t_a0, t_fill], v.quantize_mx, Zc[:, 0:128], Zs[:, 0:128], At[:, :])
+        t_h1 = run("t", [t_z] + t_ub, te.matmul_mx, T.hb[:, 0:128], T.ub[:, :], T.ubs[:, :], Zc[:, 0:128], Zs[:, 0:128], True, True)
+        t_h0 = run("t", t_ua, te.matmul_mx, T.ha[:, 0:128], T.ua[:, :], T.uas[:, :], Zc[:, 0:128], Zs[:, 0:128], True, True)
+        h1, want = F(64), F(64)
+        t_hc1 = S([t_h1], s.activation, h1, T.hb[:, 0:64], AF.Copy)
+        t_wn = V([t_h0, t_hc1], v.tensor_tensor, want, T.ha[:, 0:64], h1, A.is_gt)
+        t_sat = V([t_wn, t_c16], v.tensor_tensor_scan, sat[:, 1:65], want, c16, 0.0, A.add, A.min)
+        cown = sat[:, 64:65]
+        counts.append(cown)
+        need("g", [t_sat])
+        slots = {d: 7 - rank if rank > T.rank_of(d) else 6 - rank for d in far + [mate]}
+        g.remote_dma_fused([
+            RemoteDMATransfer(dst_ids=[did(d) for d in far], dma_engine_mask=bits(eoff), remote_sem=T.sem["ac%d" % t], srcs=[cown],
+                              dsts=[land[:, slots[d]:slots[d] + 1] for d in far]),
+            RemoteDMATransfer(dst_ids=[did(mate)], dma_engine_mask=bits(eon), remote_sem=T.sem["ac%d" % t], srcs=[cown],
+                              dsts=[land[:, slots[mate]:slots[mate] + 1]])], local_sem=T.sem.loc)
+        local += len(eoff) + len(eon)
+        hcx, stop, satm, le, encm, red = F(1), F(64), F(64), F(64), F(64), F(1)
+        sa = at["fl"]
+        seg, encw = F(64), T.fl[:, sa + 15:sa + 64:16]
+        stopw, nine, wid, wj, tww = F(4), F(4), F(4), F(4), F(4)
+        logo = O(1)
+        t_hx = V([t_sat, c_sm, t_hc], v.tensor_scalar, hcx, cown, sm, hc, A.mult, A.add)
+        t_st = V([t_sat], v.tensor_tensor, stop, sat[:, 1:65], sat[:, 0:64], A.subtract)
+        t_sm = V([c_m16], v.tensor_tensor, satm, sat[:, 1:65], m16, A.mult)
+        t_le = V([c_k], v.tensor_scalar, le, sat[:, 1:65], kcol, None, A.is_le)
+        t_em = V([t_sm, t_st], v.tensor_tensor, encm, satm, stop, A.mult)
+        t_rd = V([t_le], v.tensor_reduce, red, le, AxisListType.X, A.add)
+        t_sg = V([t_em, c_rs], v.tensor_tensor_scan, seg, rst, encm, 0.0, A.mult, A.add)
+        t_lg = V([t_rd], v.tensor_copy, logo, red)
+        t_sw = V([t_sg], v.tensor_scalar, stopw, encw, 1.0, None, A.min)
+        t_ni = V([t_sg], v.tensor_scalar, nine, encw, 9.0, None, A.is_ge)
+        t_wi = V([t_sw, c_jd], v.tensor_tensor, wid, stopw, jd, A.mult)
+        t_wj = V([t_ni, c_jw], v.tensor_tensor, wj, nine, jw, A.add)
+        t_tw = V([t_wi, t_wj], v.tensor_tensor, tww, wid, wj, A.add)
+        if t == RD - 1:
+            e6 = V([e4], v.tensor_tensor, l1, g1, jq, A.add)
+            e7 = V([e5, e6], v.tensor_tensor, l2, l1, g2, A.add)
+            t_lf = V([e7], v.tensor_copy, lfin, l2)
+        pa = at["fl"]
+        pre7, pcol, lst = F(7), T.fl[:, pa + 6:pa + 7], O(1)
+        t_p = V([("ac%d" % t, ncnt), c_m7], v.tensor_tensor_scan, pre7, land[:, 0:7], mask7, 0.0, A.add, A.mult)
+        t_ls = V([t_p, t_hx], v.tensor_scalar, lst, pcol, 0.125, hcx, A.mult, A.add)
+        t_pc = V([t_ls, t_wq, ("pre", npre)], v.tensor_copy, Zc[:, PICK:PICK + 16].bitcast(u32), T.wq[:, :].bitcast(u32).indirect(lst))
+        t_ps = S([t_ls, t_wq, ("pre", npre)], s.activation, Zs[:, PICK:PICK + 16], T.wqs[:, :].indirect(lst), AF.Copy)
+        h = len(eoff) // 4
+        ecode = [eoff[0:2 * h], eoff[2 * h:3 * h], eoff[3 * h:4 * h]]
+        escale = [eoff[0:h], eoff[2 * h:4 * h], eoff[h:2 * h]]
+        lands = [LAND + 4 * (nch - 2 - e) for e in range(nch - 1)]
+        need("g", [t_pc])
+        g.remote_dma_fused([RemoteDMATransfer(dst_ids=[did(peers[e])], dma_engine_mask=bits(ecode[e]), remote_sem=T.sem["ak%d" % t],
+                            srcs=[Zc[:, PICK + 4 * e:PICK + 4 * e + 4].bitcast(u8)], dsts=[Zc[:, lands[e]:lands[e] + 4].bitcast(u8)])
+                            for e in range(nch - 1)], local_sem=T.sem.loc)
+        need("g", [t_ps])
+        g.remote_dma_fused([RemoteDMATransfer(dst_ids=[did(peers[e])], dma_engine_mask=bits(escale[e]), remote_sem=T.sem["ap%d" % t],
+                            srcs=[Zs[:, PICK + 4 * e:PICK + 4 * e + 4]], dsts=[Zs[:, lands[e]:lands[e] + 4]])
+                            for e in range(nch - 1)], local_sem=T.sem.loc)
+        local += 2 * len(eoff)
+        bcol, vi, va, vx, vo = F(1), I(4), I(4), F(4), F(4)
+        q1, q2, q3 = F(64), F(64), F(64)
+        pl = O(4)
+        k0 = float(8 - 1 - 2 * me)
+        if rank:
+            pr = F(1)
+            t_pr = V([], v.tensor_reduce, pr, land[:, 7 - rank:7], AxisListType.X, A.add)
+            t_lcs.append(V([t_lg, t_z], v.tensor_copy, T.cc[:, 16 * t:16 * t + 16].bitcast(u32), Zc[:, 0:128].bitcast(u32).indirect(logo)))
+            t_b = V([t_pr, t_hd], v.tensor_scalar, bcol, pr, hd, k0, A.add, A.add)
+        else:
+            t_lcs.append(V([t_lg, t_z], v.tensor_copy, T.cc[:, 16 * t:16 * t + 16].bitcast(u32), Zc[:, 0:128].bitcast(u32).indirect(logo)))
+            t_b = V([t_hd], v.tensor_scalar, bcol, hd, k0, None, A.add)
+        t_lks = S([t_lg, t_z], s.activation, T.ccs[:, 16 * t:16 * t + 16], Zs[:, 0:128].indirect(logo), AF.Copy)
+        t_lis.append(V(t_num + [t_fill], v.tensor_copy, T.sidc[:, 16 * t:16 * t + 16], num[:, 0:72].indirect(logo)))
+        t_vi = V([t_b, t_sg], v.tensor_scalar, vi, encw, bcol, 2.0, A.add, A.mult)
+        f1 = V([t_b], v.tensor_scalar, q1, sat[:, 1:65], bcol, float(NR * PL - 1) - k0, A.add, A.add)
+        t_va = V([t_vi], v.tensor_scalar, va, vi, 14, None, A.bitwise_and)
+        f2 = V([f1] + t_num, v.tensor_tensor, q2, q1, num[:, 0:64], A.subtract)
+        t_vx = V([t_va, t_sw], v.tensor_tensor, vx, va, stopw, A.mult)
+        f3 = V([f2], v.tensor_tensor, q3, q2, stop, A.mult)
+        t_vo = V([t_vx, t_tw], v.tensor_tensor, vo, vx, tww, A.add)
+        t_num = [V([f3], v.tensor_tensor, numn[:, 0:64], q3, num[:, 0:64], A.add)]
+        t_pl = V([t_vo], v.tensor_copy, pl, vo)
+        if t < RD - 1:
+            tot, hdn, hcn = F(1), F(1), F(1)
+            t_to = V([], v.tensor_reduce, tot, land[:, 0:7], AxisListType.X, A.add)
+            if t == 0:
+                t_vq = V([tv], v.quantize_mx, T.vq[:, :], T.vqs[:, :], T.vt[:, :])
+            else:
+                d0, n2, d1, g1, g2, l1, l2 = F(1), F(1), F(1), F(3), F(3), F(3), F(3)
+                lfin = O(3)
+                e0 = V([], v.tensor_scalar, d0, counts[0], -1.0, 16.0, A.mult, A.add)
+                e1 = V([], v.tensor_tensor, n2, counts[0], counts[1], A.add)
+                e2 = V([], v.tensor_scalar, d1, counts[1], -1.0, 16.0, A.mult, A.add)
+            t_hd = V([t_to], v.tensor_scalar, hdn, tot, cown, hd, A.add, A.add)
+            if t:
+                e4 = V([e0, c_jw], v.tensor_scalar, g1, jq, counts[0], d0, A.is_ge, A.mult)
+                e5 = V([e1, e2], v.tensor_scalar, g2, jq, n2, d1, A.is_ge, A.mult)
+            t_hc = V([t_hd], v.tensor_scalar, hcn, hdn, 0.125, hc0, A.mult, A.add)
+            hd, hc = hdn, hcn
+        else:
+            t_l1 = V(t_lcs + [t_lf, t_pad], v.tensor_copy, T.lg[:, :].bitcast(u32), T.cc[:, :].bitcast(u32).indirect(lfin))
+            t_l2 = S([t_lks, t_lf, t_pad], s.activation, T.lgs[:, :], T.ccs[:, :].indirect(lfin), AF.Copy)
+            t_l3 = V(t_lis, v.tensor_copy, T.sidl[:, :], T.sidc[:, :].indirect(lfin))
+            dma("y", [t_l1], "st", T.oc[:, 0:192], T.lg[:, :].bitcast(u8))
+            for k in range(4):
+                dma("y", [t_l2], "st", T.osc[4 * k:4 * k + 4, 0:48], T.lgs[32 * k:32 * k + 4, :])
+            dma("y", [t_l3], "st", T.sid[0:1, 0:48], T.sidl[0:1, :])
+            dma("y", t_num, "st", T.sid[0:1, 48:112], numn[0:1, 0:64])
+        t_xc = V([t_pl, ("ak%d" % t, len(eoff)), t_z, t_pc, t_pad], v.tensor_copy, Nc[:, 0:64].bitcast(u32), Zc[:, :].bitcast(u32).indirect(pl))
+        t_xs = S([t_pl, ("ap%d" % t, len(eoff)), t_z, t_ps, t_pad], s.activation, Ns[:, 0:64], Zs[:, :].indirect(pl), AF.Copy)
+        t_X = [t_xc, t_xs]
+    t_y = run("t", t_X + [t_vq, t_pad], te.matmul_mx, T.py[:, 0:128], T.vq[:, :], T.vqs[:, :], T.x3[:, :], T.x3s[:, :], True, True)
+    dma("y", [t_xc], "st", T.oc[:, 192:448], T.x3[:, 0:64].bitcast(u8))
+    for k in range(4):
+        dma("sy"[k % 2], [t_xs], "st", T.osc[4 * k:4 * k + 4, 48:112], T.x3s[32 * k:32 * k + 4, 0:64])
+    t_yc = V([t_y], v.tensor_copy, T.ys[:, :], T.py[:, 0:64])
+    dma("y", [t_yc], "st", T.y[:, :], T.ys[:, :])
+    need("g", list(done.items()) + list(dmas.items()) + [("loc", local), ("pre", npre)] +
+         [(k + str(t), c) for t in range(RD) for k, c in (("ac", ncnt), ("ak", len(eoff)), ("ap", len(eoff)))])

@@ -3,28 +3,30 @@ from concourse.mybir import dt, AluOpType, AxisListType, ActivationFunctionType
 
 NR, PL, CS, RD = 8, 64, 16, 3
 USED = RD * CS
-PICK, SELF, LAND, ZW = 128, 140, 144, 160
+BASE, SH = 144, 9
+QW = 1 << (SH - 1)
+ZW = BASE + 3 * QW + 16
 
 SCRATCH = {
     "wt": ("sbuf", [128, 2048], "bfloat16"), "xt": ("sbuf", [128, 512], "bfloat16"),
     "qt": ("sbuf", [128, 512], "bfloat16"), "ut": ("sbuf", [128, 512], "bfloat16"), "vt": ("sbuf", [128, 512], "bfloat16"),
     "fl": ("sbuf", [128, 3000], "float32"), "il": ("sbuf", [128, 256], "int32"), "ol": ("sbuf", [128, 128], "uint16"),
-    "sidc": ("sbuf", [128, 80], "float32"), "sidl": ("sbuf", [128, 48], "float32"), "ys": ("sbuf", [128, 64], "float32"),
-    "ha": ("psum", [128, 512], "float32"), "hb": ("psum", [128, 512], "float32"), "py": ("psum", [128, 512], "float32"),
+    "sidc": ("sbuf", [128, 96], "float32"), "sidl": ("sbuf", [128, 48], "float32"), "ys": ("sbuf", [128, 64], "float32"),
+    "ha": ("psum", [128, 512], "float32"), "py": ("psum", [128, 512], "float32"),
 }
-for _n, _w in (("wc", 512), ("uq", 128), ("ua", 128), ("ub", 128), ("vq", 128), ("wq", 256), ("cc", 80), ("lg", 48),
+for _n, _w in (("wc", 512), ("uq", 128), ("ua", 128), ("ub", 128), ("vq", 128), ("wq", 256), ("cc", 128), ("lg", 48),
                ("x0", 128), ("x1", 128), ("x2", 128), ("x3", 128), ("z0", ZW), ("z1", ZW), ("z2", ZW)):
     SCRATCH[_n] = ("sbuf", [128, _w], "float8_e4m3fn_x4")
     SCRATCH[_n + "s"] = ("sbuf", [128, _w], "uint8")
 for _t in range(RD):
     SCRATCH["at%d" % _t] = ("sbuf", [128, 512], "bfloat16")
-    SCRATCH["sat%d" % _t] = ("sbuf", [128, 72], "float32")
-    SCRATCH["cnt%d" % _t] = ("sbuf", [128, 8], "float32")
+    SCRATCH["sat%d" % _t] = ("sbuf", [128, 72], "bfloat16")
+    SCRATCH["cnt%d" % _t] = ("sbuf", [128, 8], "bfloat16")
 for _t in range(RD + 1):
     SCRATCH["num%d" % _t] = ("sbuf", [128, 72], "float32")
     SCRATCH["pz%d" % _t] = ("psum", [128, 512], "float32")
-SEMAPHORES = ["vs", "ss", "ts", "gs", "lqx", "lu", "lx", "lv", "lw0", "lw1", "lw2", "lw3", "pad", "st", "pre", "loc"]
-SEMAPHORES += [k + str(t) for k in ("ac", "ak", "ap") for t in range(RD)]
+SEMAPHORES = ["vs", "ss", "ts", "gs", "lqx", "lu", "lx", "lv", "lw0", "lw1", "st", "pre", "loc"]
+SEMAPHORES += [k + str(t) for k in ("ac", "ah", "ak", "ap") for t in range(RD)]
 
 
 def rank_program(g, core, T, topo):
@@ -34,19 +36,30 @@ def rank_program(g, core, T, topo):
     A, AF = AluOpType, ActivationFunctionType
     v, s, te, sy = g.vector, g.scalar, g.tensor, g.sync
     u8, u32 = dt.uint8, dt.uint32
-    chips = []
-    for c in T.cores:
-        if not any(c in topo.cores_of(q[0]) for q in chips):
-            chips.append([d for d in T.cores if d in topo.cores_of(c)])
-    nch = len(chips)
-    me = [i for i in range(nch) if core in chips[i]][0]
-    lane = chips[me].index(core)
-    mate = chips[me][1 - lane]
-    peers = [chips[(me + 1 + e) % nch][lane] for e in range(nch - 1)]
-    far = [c for c in T.cores if c not in chips[me]]
-    eoff = topo.engines(core, far[0])
-    eon = [e for e in topo.engines(core, mate) if e not in eoff]
-    ncnt = (NR - 2) * len(eoff) + len(eon)
+
+    def quad_of(c):
+        return [d for d in T.cores if d in topo.cores_of(c) or topo.mates(c, d)]
+
+    quad = quad_of(core)
+    me = quad.index(core)
+    mate = [d for d in quad if d in topo.cores_of(core) and d != core][0]
+    side = [d for d in quad if d not in topo.cores_of(core)]
+    other = [d for d in T.cores if d not in quad]
+    twin = [d for d in other if topo.same_plane(core, d) and topo.die(d) == topo.die(core)][0]
+    half = 0 if rank < T.rank_of(twin) else 1
+    r0 = T.rank_of(quad[0])
+    peers = [quad[(me + e) % 4] for e in range(4)]
+    eoff = topo.engines(core, side[0])
+    eon = [e for e in topo.engines(core, mate) if e not in eoff][::2]
+
+    def urgent(sr, d):
+        return sr < max(T.rank_of(c) for c in quad_of(d))
+
+    def wanted(sr, d, t):
+        return t < RD - 1 or urgent(sr, d)
+
+    def early(sr, d):
+        return urgent(sr, d) or T.cores[sr] in quad_of(d)
 
     def bits(es):
         return sum(1 << e for e in es)
@@ -105,11 +118,13 @@ def rank_program(g, core, T, topo):
     def O(n):
         return take("ol", n)
 
+    tu = dma("s", [], "lu", T.ut[:, 0:8], T.u[:, 0:8])
     tqx = dma("y", [], "lqx", T.qt[:, 0:4 * USED], T.qx[:, 0:4 * USED])
-    tx = dma("s", [], "lx", T.xt[:, 0:256], T.x[:, :])
-    tu = dma("y", [], "lu", T.ut[:, 0:8], T.u[:, 0:8])
-    tw = [dma("ys"[i % 2], [], "lw%d" % i, T.wt[:, 512 * i:512 * i + 512], T.w[:, 512 * i:512 * i + 512]) for i in range(4)]
-    tv = dma("s", [], "lv", T.vt[:, :], T.v[:, :])
+    tw0 = dma("s", [], "lw0", T.wt[:, 0:1536], T.w[:, 0:1536])
+    tx = dma("y", [], "lx", T.xt[:, 0:256], T.x[:, :])
+    tw1 = dma("y", [], "lw1", T.wt[:, 1536:2048], T.w[:, 1536:2048])
+    tv = dma("y", [], "lv", T.vt[:, :], T.v[:, :])
+    tw = [tw0, tw0, tw0, tw1]
 
     def iota(out, pattern, base, cm, fl):
         if fl:
@@ -120,7 +135,7 @@ def rank_program(g, core, T, topo):
     neg, rs0, jw0 = F(7), F(64), F(4)
     ip, ip2, jp = I(1), I(1), I(64)
     t_ip = iota(ip, [[0, 1]], 0, 1, False)
-    t_ip2 = iota(ip2, [[0, 1]], 4 * (me + 1), 1, False)
+    t_ip2 = iota(ip2, [[0, 1]], 4 * me, 1, False)
     ngs = []
     if rank < NR - 1:
         ngs.append(iota(T.fl[:, a0:a0 + 7 - rank], [[1, 7 - rank]], -7, 0, True))
@@ -129,82 +144,83 @@ def rank_program(g, core, T, topo):
     t_jp = iota(jp, [[1, 64]], 0, -1, False)
     t_rs = iota(rs0, [[0, 4], [1, 16]], 0, 0, True)
     t_jw0 = iota(jw0, [[16, 4]], 0, 0, True)
-    t_num = [iota(T.num0[:, 0:64], [[1, 64]], PL * rank, 0, True)]
+    ca = at["fl"]
+    c16 = F(64)
+    t_c16 = iota(c16, [[0, 64]], 16, 0, True)
 
     t_qz = V([], v.memset, T.qt[:, 4 * USED:512], 0.0)
-    t_uz = V([], v.memset, T.ut[:, 8:512], 0.0)
     t_xz = V([], v.memset, T.xt[:, 256:512], 0.0)
+    t_uz = V([], v.memset, T.ut[:, 12:512], 0.0)
     O(16)
     V([], v.memset, T.ol[:, 0:8], 0)
-    t_lo = V([], v.memset, T.ol[:, 8:16], 1)
-    c16 = F(64)
-    t_c16 = V([], v.memset, c16, 16.0)
-    t_a0 = V([], v.memset, T.at0[:, 256:512], 0.0)
-    V([], v.memset, T.sat0[:, 0:1], 0.0)
-    hd = F(1)
-    t_hd = V([], v.memset, hd, 0.0)
-    S([t_xz], s.activation, T.at1[:, 256:512], T.xt[:, 256:512], AF.Copy)
-    S([], s.activation, T.at2[:, 256:512], T.xt[:, 256:512], AF.Copy)
-    for k in range(1, RD):
-        S([t_hd], s.activation, T["sat%d" % k][:, 0:1], hd, AF.Copy)
-    for k in range(RD):
-        S([t_c16], s.activation, T["num%d" % k][:, 64:72], T.fl[:, at["fl"] - 65:at["fl"] - 57], AF.Copy, scale=-0.0625)
-    t_fill = S([], s.activation, T.sidc[:, 48:80], T.fl[:, at["fl"] - 65:at["fl"] - 33], AF.Copy, scale=-0.0625)
+    t_lo = V([], v.memset, T.ol[:, 8:16], 2)
+    nil = T.sat0[:, 0:1]
+    t_nil = V([], v.memset, nil, 0.0)
+    t_un = S([tu], s.activation, T.ut[:, 8:12], T.ut[:, 4:8], AF.Copy, scale=-1.0)
+    t_a0 = S([t_xz], s.activation, T.at0[:, 256:512], T.xt[:, 256:512], AF.Copy)
+    rst, jd, kh, jq16, hd = F(64), F(4), F(1), F(3), F(1)
+    c_rs = S([t_rs], s.activation, rst, rs0, AF.Sign)
+    t_hd = S([t_nil], s.activation, hd, nil, AF.Copy)
 
-    ik, kcol, ic, dcol, mask7, sm = I(1), F(1), I(1), F(1), F(7), F(1)
+    ik, kcol, ic, dcol = I(1), F(1), I(1), F(1)
+    m7a = at["fl"]
+    mask7, sm = F(7), F(1)
     ih, isl, hc0a, hc0 = I(1), I(1), F(1), F(1)
-    i16, m16, rst, jd = I(64), F(64), F(64), F(4)
+    i16, m16 = I(64), F(64)
     jwa = at["fl"]
     jw = F(4)
     jq = T.fl[:, jwa:jwa + 3]
     c_ik = V([t_ip], v.tensor_scalar, ik, ip, 15, None, A.bitwise_and)
     c_ic = V([t_ip2], v.tensor_scalar, ic, ip2, 2, 3, A.logical_shift_right, A.bitwise_and)
     c_ih = V([t_ip], v.tensor_scalar, ih, ip, 1, 1, A.logical_shift_right, A.bitwise_and)
+    c_k = V([c_ik], v.tensor_copy, kcol, ik)
     c_is = V([t_ip], v.tensor_scalar, isl, ip, 1, None, A.bitwise_and)
     c_i16 = V([t_jp], v.tensor_scalar, i16, jp, 15, None, A.bitwise_and)
-    c_k = V([c_ik], v.tensor_copy, kcol, ik)
-    c_d = V([c_ic], v.tensor_scalar, dcol, ic, 2.0, float(lane), A.mult, A.add)
-    c_ha = V([c_ih], v.tensor_scalar, hc0a, ih, 128.0 - 0.125, (3.5 - 2 * me) / 8.0, A.mult, A.add)
-    c_m16 = V([c_i16], v.tensor_scalar, m16, i16, 0.0, None, A.is_equal)
-    c_rs = V([t_rs], v.tensor_scalar, rst, rs0, 1.0, None, A.min)
-    c_jw = V([t_jw0, c_k], v.tensor_scalar, jw, jw0, kcol, None, A.add)
-    c_m7 = V(ngs + [c_d], v.tensor_scalar, mask7, neg, dcol, 0.0, A.add, A.is_gt)
-    c_sm = V([c_d], v.tensor_scalar, sm, dcol, float(rank), 0.125, A.is_gt, A.mult)
-    c_hc = V([c_ha, c_is], v.tensor_tensor, hc0, hc0a, isl, A.add)
-    c_jd = V([c_jw], v.tensor_scalar, jd, jw, -1.0, float(SELF), A.mult, A.add)
 
-    wb = 128 * lane
+    wb = 128 * half
     t_wq = V([tqx, t_qz], v.quantize_mx, T.wq[:, wb:wb + 128], T.wqs[:, wb:wb + 128], T.qt[:, :])
     need("g", [t_wq])
-    rid, pid = topo.addr(mate, core)
-    g.remote_dma(T.wq[:, wb:wb + USED].bitcast(u8), T.wq[:, wb:wb + USED].bitcast(u8), T.sem.pre, T.sem.loc, pid, rid, topo.mask(core, mate))
-    g.remote_dma(T.wqs[:, wb:wb + USED], T.wqs[:, wb:wb + USED], T.sem.pre, T.sem.loc, pid, rid, topo.mask(core, mate))
-    npre = 2 * len(topo.engines(core, mate))
-    local = npre
+    rid, pid = topo.addr(twin, core)
+    g.remote_dma(T.wq[:, wb:wb + USED].bitcast(u8), T.wq[:, wb:wb + USED].bitcast(u8), T.sem.pre, T.sem.loc, pid, rid, topo.mask(core, twin))
+    g.remote_dma(T.wqs[:, wb:wb + USED], T.wqs[:, wb:wb + USED], T.sem.pre, T.sem.loc, pid, rid, topo.mask(core, twin))
+    npre = 2 * len(topo.engines(core, twin))
+    sent = [npre]
+    t_num = [iota(T.num0[:, 0:64], [[1, 64]], PL * rank, 0, True)]
+    t_fill = iota(T.sidc[:, :], [[0, 96]], -1, 0, True)
 
-    t_uq = V([tu, t_uz], v.quantize_mx, T.uq[:, :], T.uqs[:, :], T.ut[:, :])
+    t_uq = V([tu, t_uz, t_un], v.quantize_mx, T.uq[:, :], T.uqs[:, :], T.ut[:, :])
+    c_d = V([c_ic], v.tensor_scalar, dcol, ic, float(r0), None, A.add)
     t_ub = [V([t_uq, t_lo], v.tensor_copy, T.ub[:, :].bitcast(u32), T.uq[:, :].bitcast(u32).indirect(T.ol[:, 8:16])),
             S([t_uq, t_lo], s.activation, T.ubs[:, :], T.uqs[:, :].indirect(T.ol[:, 8:16]), AF.Copy)]
     t_ua = [V([], v.tensor_copy, T.ua[:, :].bitcast(u32), T.uq[:, :].bitcast(u32).indirect(T.ol[:, 0:8])),
             S([], s.activation, T.uas[:, :], T.uqs[:, :].indirect(T.ol[:, 0:8]), AF.Copy)]
-    t_X = [V([tx, t_xz], v.quantize_mx, T.x0[:, :], T.x0s[:, :], T.xt[:, :])]
-    t_w = [V([tw[i]], v.quantize_mx, T.wc[:, 128 * i:128 * i + 128], T.wcs[:, 128 * i:128 * i + 128], T.wt[:, 512 * i:512 * i + 512])
-           for i in range(4)]
-    for n in ("x1", "x2", "x3"):
-        dma("y", t_X, "pad", T[n][:, 64:128].bitcast(u8), T.x0[:, 64:128].bitcast(u8))
-        dma("y", t_X, "pad", T[n + "s"][:, 64:128], T.x0s[:, 64:128])
-    dma("y", t_X, "pad", T.cc[:, 48:80].bitcast(u8), T.x0[:, 64:96].bitcast(u8))
-    t_pad = dma("y", t_X, "pad", T.ccs[:, 48:80], T.x0s[:, 64:96])
+    c_m16 = V([c_i16], v.tensor_scalar, m16, i16, 0.0, None, A.is_equal)
+    c_jw = V([t_jw0, c_k], v.tensor_scalar, jw, jw0, kcol, None, A.add)
+    c_ha = V([c_ih], v.tensor_scalar, hc0a, ih, 128.0 - 0.5, (3.5 - me) / 8.0, A.mult, A.add)
+    c_kh = S([c_k], s.activation, kh, kcol, AF.Copy, bias=0.5)
+    c_jd = S([c_jw], s.activation, jd, jw, AF.Copy, bias=float(BASE), scale=-1.0)
+    c_j16 = S([], s.activation, jq16, jq, AF.Copy, bias=16.0)
 
-    hc, t_hc = hc0, c_hc
-    counts, t_lcs, t_lis = [], [], []
+    def quant(i):
+        return V([tw[i]], v.quantize_mx, T.wc[:, 128 * i:128 * i + 128], T.wcs[:, 128 * i:128 * i + 128], T.wt[:, 512 * i:512 * i + 512])
+
+    def zeros(n):
+        return V([t_xz], v.quantize_mx, T[n][:, :], T[n + "s"][:, :], T.xt[:, :])
+
+    t_w = [quant(0)]
+    t_X = [V([tx, t_xz], v.quantize_mx, T.x0[:, :], T.x0s[:, :], T.xt[:, :])]
+    t_w += [quant(i) for i in range(1, 4)]
+
+    hc = hc0
+    counts, t_cf, t_lcs, t_lis = [], [], [], []
+    late, ends, books = {}, [], []
     for t in range(RD):
         Xc, Xs = T["x%d" % t], T["x%ds" % t]
         Zc, Zs = T["z%d" % t], T["z%ds" % t]
         Nc, Ns = T["x%d" % (t + 1)], T["x%ds" % (t + 1)]
         At, sat, land = T["at%d" % t], T["sat%d" % t], T["cnt%d" % t]
         num, numn = T["num%d" % t], T["num%d" % (t + 1)]
-        t_mm = [run("t", t_X + [t_w[i]] + ([t_pad] if t else []), te.matmul_mx, T["pz%d" % i][:, 0:128], T.wc[:, 128 * i:128 * i + 128],
+        t_mm = [run("t", t_X + [t_w[i]], te.matmul_mx, T["pz%d" % i][:, 0:128], T.wc[:, 128 * i:128 * i + 128],
                     T.wcs[:, 128 * i:128 * i + 128], Xc[:, 0:128], Xs[:, 0:128], True, True) for i in range(4)]
         t_r = []
         for i in range(4):
@@ -213,121 +229,203 @@ def rank_program(g, core, T, topo):
                 t_r.append(V([t_mm[i]], v.tensor_scalar, o, z, 0.0, 0.0625, A.max, A.mult))
             else:
                 t_r.append(S([t_mm[i]], s.activation, o, z, AF.Relu, scale=0.0625))
-        t_z = V(t_r + [t_a0, t_fill], v.quantize_mx, Zc[:, 0:128], Zs[:, 0:128], At[:, :])
-        t_h1 = run("t", [t_z] + t_ub, te.matmul_mx, T.hb[:, 0:128], T.ub[:, :], T.ubs[:, :], Zc[:, 0:128], Zs[:, 0:128], True, True)
-        t_h0 = run("t", t_ua, te.matmul_mx, T.ha[:, 0:128], T.ua[:, :], T.uas[:, :], Zc[:, 0:128], Zs[:, 0:128], True, True)
-        h1, want = F(64), F(64)
-        t_hc1 = S([t_h1], s.activation, h1, T.hb[:, 0:64], AF.Copy)
-        t_wn = V([t_h0, t_hc1], v.tensor_tensor, want, T.ha[:, 0:64], h1, A.is_gt)
+        t_z = V(t_r + [t_a0], v.quantize_mx, Zc[:, 0:128], Zs[:, 0:128], At[:, :])
+        if t == 0:
+            c_m7 = V(ngs + [c_d], v.tensor_scalar, mask7, neg, dcol, 0.0, A.add, A.is_gt)
+            c_sm = V([c_d], v.tensor_scalar, sm, dcol, float(rank), 0.125, A.is_gt, A.mult)
+            t_hc = V([c_ha, c_is], v.tensor_tensor, hc0, hc0a, isl, A.add)
+            for k in range(RD):
+                t_nf = S([t_c16], s.activation, T["num%d" % k][:, 64:72], T.fl[:, ca:ca + 8], AF.Copy, scale=-0.0625)
+            for k in range(1, RD):
+                S([t_nil], s.activation, T["sat%d" % k][:, 0:1], nil, AF.Copy)
+            for k in range(1, RD):
+                t_a0 = S([t_xz], s.activation, T["at%d" % k][:, 256:512], T.xt[:, 256:512], AF.Copy)
+        run("t", [t_z] + t_ua, te.matmul_mx, T.ha[:, 0:128], T.ua[:, :], T.uas[:, :], Zc[:, 0:128], Zs[:, 0:128], True, False)
+        t_h = run("t", t_ub, te.matmul_mx, T.ha[:, 0:128], T.ub[:, :], T.ubs[:, :], Zc[:, 0:128], Zs[:, 0:128], False, True)
+        want, cf = F(64), F(1)
+        t_wn = V([t_h], v.tensor_scalar, want, T.ha[:, 0:64], 0.0, None, A.is_gt)
         t_sat = V([t_wn, t_c16], v.tensor_tensor_scan, sat[:, 1:65], want, c16, 0.0, A.add, A.min)
         cown = sat[:, 64:65]
-        counts.append(cown)
         need("g", [t_sat])
-        slots = {d: 7 - rank if rank > T.rank_of(d) else 6 - rank for d in far + [mate]}
-        g.remote_dma_fused([
-            RemoteDMATransfer(dst_ids=[did(d) for d in far], dma_engine_mask=bits(eoff), remote_sem=T.sem["ac%d" % t], srcs=[cown],
-                              dsts=[land[:, slots[d]:slots[d] + 1] for d in far]),
-            RemoteDMATransfer(dst_ids=[did(mate)], dma_engine_mask=bits(eon), remote_sem=T.sem["ac%d" % t], srcs=[cown],
-                              dsts=[land[:, slots[mate]:slots[mate] + 1]])], local_sem=T.sem.loc)
-        local += len(eoff) + len(eon)
-        hcx, stop, satm, le, encm, red = F(1), F(64), F(64), F(64), F(64), F(1)
+        slots = {d: 7 - rank if rank > T.rank_of(d) else 6 - rank for d in side + [mate] + other}
+
+        def give(ds, es):
+            ds = [d for d in ds if wanted(rank, d, t)]
+            if not ds:
+                return []
+            sent.append(len(es))
+            sem = T.sem[("ac%d" if early(rank, ds[0]) else "ah%d") % t]
+            return [RemoteDMATransfer(dst_ids=[did(d) for d in ds], dma_engine_mask=bits(es), remote_sem=sem, srcs=[cown],
+                                      dsts=[land[:, slots[d]:slots[d] + 1] for d in ds])]
+
+        ahead = urgent(rank, other[0])
+        now = give(side + other if ahead else side, eoff) + give([mate], eon)
+        tail = [] if ahead else give(other, eoff)
+        if now:
+            g.remote_dma_fused(now, local_sem=T.sem.loc)
+        inc = {d: len(eon) if d == mate else len(eoff) for d in side + [mate] + other if wanted(T.rank_of(d), core, t)}
+        soon = [d for d in inc if early(T.rank_of(d), core)]
+        na, nac = len(soon), sum(inc[d] for d in soon)
+        nah = sum(inc.values()) - nac
+        hcx, stop, satm, encm, sgn, red = F(1), F(64), F(64), F(64), F(64), F(1)
         sa = at["fl"]
         seg, encw = F(64), T.fl[:, sa + 15:sa + 64:16]
-        stopw, nine, wid, wj, tww = F(4), F(4), F(4), F(4), F(4)
+        stopw, nine, wid, wj, tww, hdk, bcol = F(4), F(4), F(4), F(4), F(4), F(1), F(1)
         logo = O(1)
-        t_hx = V([t_sat, c_sm, t_hc], v.tensor_scalar, hcx, cown, sm, hc, A.mult, A.add)
+        t_rd = S([t_sat, c_kh], s.activation, sgn, sat[:, 1:65], AF.Sign, bias=kh, scale=-1.0, accum_out=red)
+        t_cf.append(S([t_sat], s.activation, cf, cown, AF.Copy))
+        counts.append(cf)
+        if t:
+            tot, hdn, hcn = F(1), F(1), F(1)
+            t_to = V(late[t - 1], v.tensor_reduce, tot, T["cnt%d" % (t - 1)][:, 0:7], AxisListType.X, A.add)
         t_st = V([t_sat], v.tensor_tensor, stop, sat[:, 1:65], sat[:, 0:64], A.subtract)
+        if t:
+            t_hd = V([t_to, t_hd, t_cf[t - 1]], v.tensor_scalar, hdn, tot, counts[t - 1], hd, A.add, A.add)
         t_sm = V([c_m16], v.tensor_tensor, satm, sat[:, 1:65], m16, A.mult)
-        t_le = V([c_k], v.tensor_scalar, le, sat[:, 1:65], kcol, None, A.is_le)
+        if t:
+            t_hc = V([t_hd], v.tensor_scalar, hcn, hdn, 0.125, hc0, A.mult, A.add)
+            hd, hc = hdn, hcn
+        t_hk = V([t_hd], v.tensor_scalar, hdk, hd, float(NR - 1), None, A.add)
         t_em = V([t_sm, t_st], v.tensor_tensor, encm, satm, stop, A.mult)
-        t_rd = V([t_le], v.tensor_reduce, red, le, AxisListType.X, A.add)
+        t_hx = V([t_sat, c_sm, t_hc], v.tensor_scalar, hcx, cown, sm, hc, A.mult, A.add)
+        for f in books[:2]:
+            f()
         t_sg = V([t_em, c_rs], v.tensor_tensor_scan, seg, rst, encm, 0.0, A.mult, A.add)
-        t_lg = V([t_rd], v.tensor_copy, logo, red)
+        for f in books[2:4]:
+            f()
         t_sw = V([t_sg], v.tensor_scalar, stopw, encw, 1.0, None, A.min)
         t_ni = V([t_sg], v.tensor_scalar, nine, encw, 9.0, None, A.is_ge)
-        t_wi = V([t_sw, c_jd], v.tensor_tensor, wid, stopw, jd, A.mult)
-        t_wj = V([t_ni, c_jw], v.tensor_tensor, wj, nine, jw, A.add)
-        t_tw = V([t_wi, t_wj], v.tensor_tensor, tww, wid, wj, A.add)
-        if t == RD - 1:
-            e6 = V([e4], v.tensor_tensor, l1, g1, jq, A.add)
-            e7 = V([e5, e6], v.tensor_tensor, l2, l1, g2, A.add)
-            t_lf = V([e7], v.tensor_copy, lfin, l2)
+        if t == 0:
+            t_xp = [zeros("x1")]
+            t_cz = zeros("cc")
+            t_xp.append(zeros("x2"))
         pa = at["fl"]
-        pre7, pcol, lst = F(7), T.fl[:, pa + 6:pa + 7], O(1)
-        t_p = V([("ac%d" % t, ncnt), c_m7], v.tensor_tensor_scan, pre7, land[:, 0:7], mask7, 0.0, A.add, A.mult)
+        pre, pcol, lst = F(na), T.fl[:, pa + na - 1:pa + na], O(1)
+        mask = T.fl[:, m7a + 7 - na:m7a + 7]
+        P = BASE + QW * me
+        ac = ("ac%d" % t, nac)
+        late[t] = [ac] + ([("ah%d" % t, nah)] if nah else [])
+        t_p = V([ac, c_m7], v.tensor_tensor_scan, pre, land[:, 7 - na:7], mask, 0.0, A.add, A.mult)
         t_ls = V([t_p, t_hx], v.tensor_scalar, lst, pcol, 0.125, hcx, A.mult, A.add)
-        t_pc = V([t_ls, t_wq, ("pre", npre)], v.tensor_copy, Zc[:, PICK:PICK + 16].bitcast(u32), T.wq[:, :].bitcast(u32).indirect(lst))
-        t_ps = S([t_ls, t_wq, ("pre", npre)], s.activation, Zs[:, PICK:PICK + 16], T.wqs[:, :].indirect(lst), AF.Copy)
-        h = len(eoff) // 4
-        ecode = [eoff[0:2 * h], eoff[2 * h:3 * h], eoff[3 * h:4 * h]]
-        escale = [eoff[0:h], eoff[2 * h:4 * h], eoff[h:2 * h]]
-        lands = [LAND + 4 * (nch - 2 - e) for e in range(nch - 1)]
-        need("g", [t_pc])
-        g.remote_dma_fused([RemoteDMATransfer(dst_ids=[did(peers[e])], dma_engine_mask=bits(ecode[e]), remote_sem=T.sem["ak%d" % t],
-                            srcs=[Zc[:, PICK + 4 * e:PICK + 4 * e + 4].bitcast(u8)], dsts=[Zc[:, lands[e]:lands[e] + 4].bitcast(u8)])
-                            for e in range(nch - 1)], local_sem=T.sem.loc)
-        need("g", [t_ps])
-        g.remote_dma_fused([RemoteDMATransfer(dst_ids=[did(peers[e])], dma_engine_mask=bits(escale[e]), remote_sem=T.sem["ap%d" % t],
-                            srcs=[Zs[:, PICK + 4 * e:PICK + 4 * e + 4]], dsts=[Zs[:, lands[e]:lands[e] + 4]])
-                            for e in range(nch - 1)], local_sem=T.sem.loc)
-        local += 2 * len(eoff)
-        bcol, vi, va, vx, vo = F(1), I(4), I(4), F(4), F(4)
-        q1, q2, q3 = F(64), F(64), F(64)
+        t_pc = V([t_ls, t_wq, ("pre", npre)], v.tensor_copy, Zc[:, P:P + 16].bitcast(u32), T.wq[:, :].bitcast(u32).indirect(lst))
+        t_ps = S([t_ls, t_wq, ("pre", npre)], s.activation, Zs[:, P:P + 16], T.wqs[:, :].indirect(lst), AF.Copy)
+
+        def codes(via):
+            return [RemoteDMATransfer(dst_ids=[did(peers[e])], dma_engine_mask=bits(via[peers[e]]), remote_sem=T.sem["ak%d" % t],
+                                      srcs=[Zc[:, P + 4 * e:P + 4 * e + 4].bitcast(u8)], dsts=[Zc[:, P:P + 4].bitcast(u8)])
+                    for e in range(1, 4)]
+
+        def scales(via, w):
+            out = []
+            for e in range(1, 4):
+                o = 4 * e if w == 4 else 0
+                out.append(RemoteDMATransfer(dst_ids=[did(peers[e])], dma_engine_mask=bits(via[peers[e]]), remote_sem=T.sem["ap%d" % t],
+                                             srcs=[Zs[:, P + o:P + o + w]], dsts=[Zs[:, P + o - 4 * e:P + o - 4 * e + w]]))
+            return out
+
+        h = len(eon) // 2
+        if t < RD - 1:
+            need("g", [t_pc, t_ps])
+            g.remote_dma_fused(codes({side[0]: eoff[:h], side[1]: eoff[h:2 * h], mate: eon[:h]}) +
+                               scales({side[0]: eoff[2 * h:3 * h], side[1]: eoff[3 * h:], mate: eon[h:]}, 16), local_sem=T.sem.loc)
+            ncol = 3 * h
+        else:
+            via = {side[0]: eoff[:2 * h], side[1]: eoff[2 * h:], mate: eon}
+            need("g", [t_pc])
+            g.remote_dma_fused(codes(via), local_sem=T.sem.loc)
+            need("g", [t_ps])
+            g.remote_dma_fused(scales(via, 4), local_sem=T.sem.loc)
+            ncol = 6 * h
+        sent.append(2 * ncol)
+        if tail:
+            g.remote_dma_fused(tail, local_sem=T.sem.loc)
+        ends += [("ak%d" % t, ncol), ("ap%d" % t, ncol)] + late[t]
+        vi, va, vx, vo = I(4), I(4), F(4), F(4)
+        q = (F(64), F(64), F(64))
         pl = O(4)
-        k0 = float(8 - 1 - 2 * me)
+        t_b = t_hk
         if rank:
             pr = F(1)
             t_pr = V([], v.tensor_reduce, pr, land[:, 7 - rank:7], AxisListType.X, A.add)
-            t_lcs.append(V([t_lg, t_z], v.tensor_copy, T.cc[:, 16 * t:16 * t + 16].bitcast(u32), Zc[:, 0:128].bitcast(u32).indirect(logo)))
-            t_b = V([t_pr, t_hd], v.tensor_scalar, bcol, pr, hd, k0, A.add, A.add)
+        t_wj = V([t_ni, c_jw], v.tensor_tensor, wj, nine, jw, A.add)
+        t_lg = V([t_rd], v.tensor_scalar, logo, red, 0.5, 32.0, A.mult, A.add)
+        if rank:
+            t_b = V([t_hk, t_pr], v.tensor_tensor, bcol, hdk, pr, A.add)
         else:
-            t_lcs.append(V([t_lg, t_z], v.tensor_copy, T.cc[:, 16 * t:16 * t + 16].bitcast(u32), Zc[:, 0:128].bitcast(u32).indirect(logo)))
-            t_b = V([t_hd], v.tensor_scalar, bcol, hd, k0, None, A.add)
-        t_lks = S([t_lg, t_z], s.activation, T.ccs[:, 16 * t:16 * t + 16], Zs[:, 0:128].indirect(logo), AF.Copy)
-        t_lis.append(V(t_num + [t_fill], v.tensor_copy, T.sidc[:, 16 * t:16 * t + 16], num[:, 0:72].indirect(logo)))
-        t_vi = V([t_b, t_sg], v.tensor_scalar, vi, encw, bcol, 2.0, A.add, A.mult)
-        f1 = V([t_b], v.tensor_scalar, q1, sat[:, 1:65], bcol, float(NR * PL - 1) - k0, A.add, A.add)
-        t_va = V([t_vi], v.tensor_scalar, va, vi, 14, None, A.bitwise_and)
-        f2 = V([f1] + t_num, v.tensor_tensor, q2, q1, num[:, 0:64], A.subtract)
+            bcol = hdk
+        t_wi = V([t_sw, c_jd], v.tensor_tensor, wid, stopw, jd, A.mult)
+        t_vi = V([t_b, t_sg], v.tensor_scalar, vi, encw, bcol, float(2 ** SH + 1), A.add, A.mult)
+        t_tw = V([t_wi, t_wj], v.tensor_tensor, tww, wid, wj, A.add)
+        t_va = V([t_vi], v.tensor_scalar, va, vi, 1, 3 * QW + 2, A.logical_shift_right, A.bitwise_and)
+        for f in books[4:5]:
+            f()
         t_vx = V([t_va, t_sw], v.tensor_tensor, vx, va, stopw, A.mult)
-        f3 = V([f2], v.tensor_tensor, q3, q2, stop, A.mult)
         t_vo = V([t_vx, t_tw], v.tensor_tensor, vo, vx, tww, A.add)
-        t_num = [V([f3], v.tensor_tensor, numn[:, 0:64], q3, num[:, 0:64], A.add)]
+        for f in books[5:]:
+            f()
         t_pl = V([t_vo], v.tensor_copy, pl, vo)
-        if t < RD - 1:
-            tot, hdn, hcn = F(1), F(1), F(1)
-            t_to = V([], v.tensor_reduce, tot, land[:, 0:7], AxisListType.X, A.add)
-            if t == 0:
-                t_vq = V([tv], v.quantize_mx, T.vq[:, :], T.vqs[:, :], T.vt[:, :])
-            else:
-                d0, n2, d1, g1, g2, l1, l2 = F(1), F(1), F(1), F(3), F(3), F(3), F(3)
-                lfin = O(3)
-                e0 = V([], v.tensor_scalar, d0, counts[0], -1.0, 16.0, A.mult, A.add)
-                e1 = V([], v.tensor_tensor, n2, counts[0], counts[1], A.add)
-                e2 = V([], v.tensor_scalar, d1, counts[1], -1.0, 16.0, A.mult, A.add)
-            t_hd = V([t_to], v.tensor_scalar, hdn, tot, cown, hd, A.add, A.add)
-            if t:
-                e4 = V([e0, c_jw], v.tensor_scalar, g1, jq, counts[0], d0, A.is_ge, A.mult)
-                e5 = V([e1, e2], v.tensor_scalar, g2, jq, n2, d1, A.is_ge, A.mult)
-            t_hc = V([t_hd], v.tensor_scalar, hcn, hdn, 0.125, hc0, A.mult, A.add)
-            hd, hc = hdn, hcn
-        else:
-            t_l1 = V(t_lcs + [t_lf, t_pad], v.tensor_copy, T.lg[:, :].bitcast(u32), T.cc[:, :].bitcast(u32).indirect(lfin))
-            t_l2 = S([t_lks, t_lf, t_pad], s.activation, T.lgs[:, :], T.ccs[:, :].indirect(lfin), AF.Copy)
-            t_l3 = V(t_lis, v.tensor_copy, T.sidl[:, :], T.sidc[:, :].indirect(lfin))
+        if t == 0:
+            t_xp.append(zeros("x3"))
+            t_vq = V([tv], v.quantize_mx, T.vq[:, :], T.vqs[:, :], T.vt[:, :])
+        ra = 16 + 16 * t
+        t_lks = S([t_lg, t_z, t_cz], s.activation, T.ccs[:, ra:ra + 16], Zs[:, 0:128].indirect(logo), AF.Copy)
+
+        def book(bcol=bcol, t_b=t_b, q=q, t_lg=t_lg, t_z=t_z, t_st=t_st, stop=stop, sat=sat, num=num, numn=numn, ra=ra, logo=logo, Zc=Zc):
+            k = {}
+
+            def b0():
+                t_lcs.append(V([t_lg, t_z, t_cz], v.tensor_copy, T.cc[:, ra:ra + 16].bitcast(u32), Zc[:, 0:128].bitcast(u32).indirect(logo)))
+
+            def b1():
+                k[1] = V([t_b], v.tensor_scalar, q[0], sat[:, 1:65], bcol, float(NR * PL - NR), A.add, A.add)
+
+            def b2():
+                t_lis.append(V(t_num + [t_fill, t_nf], v.tensor_copy, T.sidc[:, ra:ra + 16], num[:, 0:72].indirect(logo)))
+
+            def b3():
+                k[2] = V([k[1]] + t_num, v.tensor_tensor, q[1], q[0], num[:, 0:64], A.subtract)
+
+            def b4():
+                k[3] = V([k[2], t_st], v.tensor_tensor, q[2], q[1], stop, A.mult)
+
+            def b5():
+                t_num[:] = [V([k[3]], v.tensor_tensor, numn[:, 0:64], q[2], num[:, 0:64], A.add)]
+
+            return [b0, b1, b2, b3, b4, b5]
+
+        books = book()
+        if t == RD - 2:
+            d0, n2, d1, g1, g2, l1, l2 = F(1), F(1), F(1), F(3), F(3), F(3), F(3)
+            lfin = O(3)
+            e0 = V([t_cf[1]], v.tensor_scalar, d0, counts[0], -1.0, 16.0, A.mult, A.add)
+            e1 = V([], v.tensor_tensor, n2, counts[0], counts[1], A.add)
+            e2 = V([], v.tensor_scalar, d1, counts[1], -1.0, 16.0, A.mult, A.add)
+            e4 = V([e0, c_jw], v.tensor_scalar, g1, jq, counts[0], d0, A.is_ge, A.mult)
+            e5 = V([e1, e2], v.tensor_scalar, g2, jq, n2, d1, A.is_ge, A.mult)
+            e6 = V([e4, c_j16], v.tensor_tensor, l1, g1, jq16, A.add)
+            e7 = V([e5, e6], v.tensor_tensor, l2, l1, g2, A.add)
+            t_lf = V([e7], v.tensor_copy, lfin, l2)
+        if t == RD - 1:
+            books[0]()
+            t_l2 = S([t_lks, t_lf], s.activation, T.lgs[:, :], T.ccs[:, :].indirect(lfin), AF.Copy)
+            t_l1 = V(t_lcs + [t_lf], v.tensor_copy, T.lg[:, :].bitcast(u32), T.cc[:, :].bitcast(u32).indirect(lfin))
             dma("y", [t_l1], "st", T.oc[:, 0:192], T.lg[:, :].bitcast(u8))
             for k in range(4):
                 dma("y", [t_l2], "st", T.osc[4 * k:4 * k + 4, 0:48], T.lgs[32 * k:32 * k + 4, :])
-            dma("y", [t_l3], "st", T.sid[0:1, 0:48], T.sidl[0:1, :])
-            dma("y", t_num, "st", T.sid[0:1, 48:112], numn[0:1, 0:64])
-        t_xc = V([t_pl, ("ak%d" % t, len(eoff)), t_z, t_pc, t_pad], v.tensor_copy, Nc[:, 0:64].bitcast(u32), Zc[:, :].bitcast(u32).indirect(pl))
-        t_xs = S([t_pl, ("ap%d" % t, len(eoff)), t_z, t_ps, t_pad], s.activation, Ns[:, 0:64], Zs[:, :].indirect(pl), AF.Copy)
+        t_xc = V([t_pl, ("ak%d" % t, ncol), t_z, t_pc, t_xp[t]], v.tensor_copy, Nc[:, 0:64].bitcast(u32), Zc[:, :].bitcast(u32).indirect(pl))
+        t_xs = S([t_pl, ("ap%d" % t, ncol), t_z, t_ps, t_xp[t]], s.activation, Ns[:, 0:64], Zs[:, :].indirect(pl), AF.Copy)
         t_X = [t_xc, t_xs]
-    t_y = run("t", t_X + [t_vq, t_pad], te.matmul_mx, T.py[:, 0:128], T.vq[:, :], T.vqs[:, :], T.x3[:, :], T.x3s[:, :], True, True)
+    t_y = run("t", t_X + [t_vq], te.matmul_mx, T.py[:, 0:128], T.vq[:, :], T.vqs[:, :], T.x3[:, :], T.x3s[:, :], True, True)
     dma("y", [t_xc], "st", T.oc[:, 192:448], T.x3[:, 0:64].bitcast(u8))
     for k in range(4):
         dma("sy"[k % 2], [t_xs], "st", T.osc[4 * k:4 * k + 4, 48:112], T.x3s[32 * k:32 * k + 4, 0:64])
-    t_yc = V([t_y], v.tensor_copy, T.ys[:, :], T.py[:, 0:64])
-    dma("y", [t_yc], "st", T.y[:, :], T.ys[:, :])
-    need("g", list(done.items()) + list(dmas.items()) + [("loc", local), ("pre", npre)] +
-         [(k + str(t), c) for t in range(RD) for k, c in (("ac", ncnt), ("ak", len(eoff)), ("ap", len(eoff)))])
+    t_yc = S([t_y], s.activation, T.ys[:, :], T.py[:, 0:64], AF.Copy)
+    for f in books[1:4]:
+        f()
+    t_l3 = V(t_lis, v.tensor_copy, T.sidl[:, :], T.sidc[:, :].indirect(lfin))
+    for f in books[4:]:
+        f()
+    dma("y", [t_l3], "st", T.sid[0:1, 0:48], T.sidl[0:1, :])
+    dma("s", [t_yc], "st", T.y[:, :], T.ys[:, :])
+    dma("y", t_num, "st", T.sid[0:1, 48:112], T["num%d" % RD][0:1, 0:64])
+    need("g", list(done.items()) + list(dmas.items()) + [("loc", sum(sent)), ("pre", npre)] + ends)

from concourse.bass import DstId, RemoteDMATransfer
from concourse.mybir import dt, AluOpType, AxisListType, ActivationFunctionType

NR, PL, CS, RD = 8, 64, 16, 3
USED = RD * CS
BASE, SH = 144, 9
QW = 1 << (SH - 1)
ZW = BASE + 3 * QW + 16

SCRATCH = {
    "wt": ("sbuf", [128, 2048], "bfloat16"), "xt": ("sbuf", [128, 512], "bfloat16"),
    "qt": ("sbuf", [128, 512], "bfloat16"), "ut": ("sbuf", [128, 512], "bfloat16"), "vt": ("sbuf", [128, 512], "bfloat16"),
    "fl": ("sbuf", [128, 3000], "float32"), "il": ("sbuf", [128, 256], "int32"), "ol": ("sbuf", [128, 128], "uint16"),
    "sidc": ("sbuf", [128, 96], "float32"), "sidl": ("sbuf", [128, 48], "float32"), "ys": ("sbuf", [128, 64], "float32"),
    "ha": ("psum", [128, 512], "float32"), "py": ("psum", [128, 512], "float32"),
}
for _n, _w in (("wc", 512), ("uq", 128), ("ua", 128), ("ub", 128), ("vq", 128), ("wq", 256), ("cc", 128), ("lg", 48),
               ("x0", 128), ("x1", 128), ("x2", 128), ("x3", 128), ("z0", ZW), ("z1", ZW), ("z2", ZW)):
    SCRATCH[_n] = ("sbuf", [128, _w], "float8_e4m3fn_x4")
    SCRATCH[_n + "s"] = ("sbuf", [128, _w], "uint8")
for _t in range(RD):
    SCRATCH["at%d" % _t] = ("sbuf", [128, 512], "bfloat16")
    SCRATCH["sat%d" % _t] = ("sbuf", [128, 72], "bfloat16")
    SCRATCH["cnt%d" % _t] = ("sbuf", [128, 8], "bfloat16")
for _t in range(RD + 1):
    SCRATCH["num%d" % _t] = ("sbuf", [128, 72], "float32")
    SCRATCH["pz%d" % _t] = ("psum", [128, 512], "float32")
SEMAPHORES = ["vs", "ss", "ts", "gs", "lqx", "lu", "lx", "lv", "lw0", "lw1", "st", "pre", "loc"]
SEMAPHORES += [k + str(t) for k in ("ac", "ah", "ak", "ap") for t in range(RD)]


def rank_program(g, core, T, topo):
    rank = T.rank_of(core)
    if rank is None:
        return
    A, AF = AluOpType, ActivationFunctionType
    v, s, te, sy = g.vector, g.scalar, g.tensor, g.sync
    u8, u32 = dt.uint8, dt.uint32

    def quad_of(c):
        return [d for d in T.cores if d in topo.cores_of(c) or topo.mates(c, d)]

    quad = quad_of(core)
    me = quad.index(core)
    mate = [d for d in quad if d in topo.cores_of(core) and d != core][0]
    side = [d for d in quad if d not in topo.cores_of(core)]
    other = [d for d in T.cores if d not in quad]
    twin = [d for d in other if topo.same_plane(core, d) and topo.die(d) == topo.die(core)][0]
    half = 0 if rank < T.rank_of(twin) else 1
    r0 = T.rank_of(quad[0])
    peers = [quad[(me + e) % 4] for e in range(4)]
    eoff = topo.engines(core, side[0])
    eon = [e for e in topo.engines(core, mate) if e not in eoff][::2]

    def urgent(sr, d):
        return sr < max(T.rank_of(c) for c in quad_of(d))

    def wanted(sr, d, t):
        return t < RD - 1 or urgent(sr, d)

    def early(sr, d):
        return urgent(sr, d) or T.cores[sr] in quad_of(d)

    def bits(es):
        return sum(1 << e for e in es)

    def did(d):
        rid, pid = topo.addr(d, core)
        return DstId(rid=rid, pnc=pid)

    Q = {"v": v, "s": s, "t": te, "g": g, "y": sy}
    own = {"v": "vs", "s": "ss", "t": "ts", "g": "gs"}
    done = {"vs": 0, "ss": 0, "ts": 0, "gs": 0}
    dmas = {}
    seen = {q: {} for q in Q}

    def need(q, deps):
        top = {}
        for n, c in deps:
            top[n] = max(top.get(n, 0), c)
        for n, c in top.items():
            if seen[q].get(n, 0) < c:
                Q[q].wait_ge(T.sem[n], c)
                seen[q][n] = c

    def run(q, deps, call, *a, **k):
        need(q, deps)
        n = own[q]
        call(*a, **k).then_inc(T.sem[n], 1)
        done[n] += 1
        return (n, done[n])

    def V(deps, call, *a, **k):
        return run("v", deps, call, *a, **k)

    def S(deps, call, *a, **k):
        return run("s", deps, call, *a, **k)

    def dma(q, deps, sem, out, in_):
        need(q, deps)
        Q[q].dma_start(out, in_).then_inc(T.sem[sem], 16)
        dmas[sem] = dmas.get(sem, 0) + 16
        return (sem, dmas[sem])

    at = {"fl": 0, "il": 0, "ol": 0}

    def take(buf, n):
        a = at[buf]
        at[buf] = a + n + (n % 2 if buf == "ol" else 0)
        return T[buf][:, a:a + n]

    def F(n):
        return take("fl", n)

    def I(n):
        return take("il", n)

    def O(n):
        return take("ol", n)

    tu = dma("s", [], "lu", T.ut[:, 0:8], T.u[:, 0:8])
    tqx = dma("y", [], "lqx", T.qt[:, 0:4 * USED], T.qx[:, 0:4 * USED])
    tw0 = dma("s", [], "lw0", T.wt[:, 0:1536], T.w[:, 0:1536])
    tx = dma("y", [], "lx", T.xt[:, 0:256], T.x[:, :])
    tw1 = dma("y", [], "lw1", T.wt[:, 1536:2048], T.w[:, 1536:2048])
    tv = dma("y", [], "lv", T.vt[:, :], T.v[:, :])
    tw = [tw0, tw0, tw0, tw1]

    def iota(out, pattern, base, cm, fl):
        if fl:
            return run("g", [], g.iota, out, pattern, base, cm, allow_small_or_imprecise_dtypes=True)
        return run("g", [], g.iota, out, pattern, base, cm)

    a0 = at["fl"]
    neg, rs0, jw0 = F(7), F(64), F(4)
    ip, ip2, jp = I(1), I(1), I(64)
    t_ip = iota(ip, [[0, 1]], 0, 1, False)
    t_ip2 = iota(ip2, [[0, 1]], 4 * me, 1, False)
    ngs = []
    if rank < NR - 1:
        ngs.append(iota(T.fl[:, a0:a0 + 7 - rank], [[1, 7 - rank]], -7, 0, True))
    if rank > 0:
        ngs.append(iota(T.fl[:, a0 + 7 - rank:a0 + 7], [[1, rank]], 1 - rank, 0, True))
    t_jp = iota(jp, [[1, 64]], 0, -1, False)
    t_rs = iota(rs0, [[0, 4], [1, 16]], 0, 0, True)
    t_jw0 = iota(jw0, [[16, 4]], 0, 0, True)
    ca = at["fl"]
    c16 = F(64)
    t_c16 = iota(c16, [[0, 64]], 16, 0, True)

    t_qz = V([], v.memset, T.qt[:, 4 * USED:512], 0.0)
    t_xz = V([], v.memset, T.xt[:, 256:512], 0.0)
    t_uz = V([], v.memset, T.ut[:, 12:512], 0.0)
    O(16)
    V([], v.memset, T.ol[:, 0:8], 0)
    t_lo = V([], v.memset, T.ol[:, 8:16], 2)
    nil = T.sat0[:, 0:1]
    t_nil = V([], v.memset, nil, 0.0)
    t_un = S([tu], s.activation, T.ut[:, 8:12], T.ut[:, 4:8], AF.Copy, scale=-1.0)
    t_a0 = S([t_xz], s.activation, T.at0[:, 256:512], T.xt[:, 256:512], AF.Copy)
    rst, jd, kh, jq16, hd = F(64), F(4), F(1), F(3), F(1)
    c_rs = S([t_rs], s.activation, rst, rs0, AF.Sign)
    t_hd = S([t_nil], s.activation, hd, nil, AF.Copy)

    ik, kcol, ic, dcol = I(1), F(1), I(1), F(1)
    m7a = at["fl"]
    mask7, sm = F(7), F(1)
    ih, isl, hc0a, hc0 = I(1), I(1), F(1), F(1)
    i16, m16 = I(64), F(64)
    jwa = at["fl"]
    jw = F(4)
    jq = T.fl[:, jwa:jwa + 3]
    c_ik = V([t_ip], v.tensor_scalar, ik, ip, 15, None, A.bitwise_and)
    c_ic = V([t_ip2], v.tensor_scalar, ic, ip2, 2, 3, A.logical_shift_right, A.bitwise_and)
    c_ih = V([t_ip], v.tensor_scalar, ih, ip, 1, 1, A.logical_shift_right, A.bitwise_and)
    c_k = V([c_ik], v.tensor_copy, kcol, ik)
    c_is = V([t_ip], v.tensor_scalar, isl, ip, 1, None, A.bitwise_and)
    c_i16 = V([t_jp], v.tensor_scalar, i16, jp, 15, None, A.bitwise_and)

    wb = 128 * half
    t_wq = V([tqx, t_qz], v.quantize_mx, T.wq[:, wb:wb + 128], T.wqs[:, wb:wb + 128], T.qt[:, :])
    need("g", [t_wq])
    rid, pid = topo.addr(twin, core)
    g.remote_dma(T.wq[:, wb:wb + USED].bitcast(u8), T.wq[:, wb:wb + USED].bitcast(u8), T.sem.pre, T.sem.loc, pid, rid, topo.mask(core, twin))
    g.remote_dma(T.wqs[:, wb:wb + USED], T.wqs[:, wb:wb + USED], T.sem.pre, T.sem.loc, pid, rid, topo.mask(core, twin))
    npre = 2 * len(topo.engines(core, twin))
    sent = [npre]
    t_num = [iota(T.num0[:, 0:64], [[1, 64]], PL * rank, 0, True)]
    t_fill = iota(T.sidc[:, :], [[0, 96]], -1, 0, True)

    t_uq = V([tu, t_uz, t_un], v.quantize_mx, T.uq[:, :], T.uqs[:, :], T.ut[:, :])
    c_d = V([c_ic], v.tensor_scalar, dcol, ic, float(r0), None, A.add)
    t_ub = [V([t_uq, t_lo], v.tensor_copy, T.ub[:, :].bitcast(u32), T.uq[:, :].bitcast(u32).indirect(T.ol[:, 8:16])),
            S([t_uq, t_lo], s.activation, T.ubs[:, :], T.uqs[:, :].indirect(T.ol[:, 8:16]), AF.Copy)]
    t_ua = [V([], v.tensor_copy, T.ua[:, :].bitcast(u32), T.uq[:, :].bitcast(u32).indirect(T.ol[:, 0:8])),
            S([], s.activation, T.uas[:, :], T.uqs[:, :].indirect(T.ol[:, 0:8]), AF.Copy)]
    c_m16 = V([c_i16], v.tensor_scalar, m16, i16, 0.0, None, A.is_equal)
    c_jw = V([t_jw0, c_k], v.tensor_scalar, jw, jw0, kcol, None, A.add)
    c_ha = V([c_ih], v.tensor_scalar, hc0a, ih, 128.0 - 0.5, (3.5 - me) / 8.0, A.mult, A.add)
    c_kh = S([c_k], s.activation, kh, kcol, AF.Copy, bias=0.5)
    c_jd = S([c_jw], s.activation, jd, jw, AF.Copy, bias=float(BASE), scale=-1.0)
    c_j16 = S([], s.activation, jq16, jq, AF.Copy, bias=16.0)

    def quant(i):
        return V([tw[i]], v.quantize_mx, T.wc[:, 128 * i:128 * i + 128], T.wcs[:, 128 * i:128 * i + 128], T.wt[:, 512 * i:512 * i + 512])

    def zeros(n):
        return V([t_xz], v.quantize_mx, T[n][:, :], T[n + "s"][:, :], T.xt[:, :])

    t_w = [quant(0)]
    t_X = [V([tx, t_xz], v.quantize_mx, T.x0[:, :], T.x0s[:, :], T.xt[:, :])]
    t_w += [quant(i) for i in range(1, 4)]

    hc = hc0
    counts, t_cf, t_lcs, t_lis = [], [], [], []
    late, ends, books = {}, [], []
    for t in range(RD):
        Xc, Xs = T["x%d" % t], T["x%ds" % t]
        Zc, Zs = T["z%d" % t], T["z%ds" % t]
        Nc, Ns = T["x%d" % (t + 1)], T["x%ds" % (t + 1)]
        At, sat, land = T["at%d" % t], T["sat%d" % t], T["cnt%d" % t]
        num, numn = T["num%d" % t], T["num%d" % (t + 1)]
        t_mm = [run("t", t_X + [t_w[i]], te.matmul_mx, T["pz%d" % i][:, 0:128], T.wc[:, 128 * i:128 * i + 128],
                    T.wcs[:, 128 * i:128 * i + 128], Xc[:, 0:128], Xs[:, 0:128], True, True) for i in range(4)]
        t_r = []
        for i in range(4):
            o, z = At[:, i:256:4], T["pz%d" % i][:, 0:64]
            if i % 2:
                t_r.append(V([t_mm[i]], v.tensor_scalar, o, z, 0.0, 0.0625, A.max, A.mult))
            else:
                t_r.append(S([t_mm[i]], s.activation, o, z, AF.Relu, scale=0.0625))
        t_z = V(t_r + [t_a0], v.quantize_mx, Zc[:, 0:128], Zs[:, 0:128], At[:, :])
        if t == 0:
            c_m7 = V(ngs + [c_d], v.tensor_scalar, mask7, neg, dcol, 0.0, A.add, A.is_gt)
            c_sm = V([c_d], v.tensor_scalar, sm, dcol, float(rank), 0.125, A.is_gt, A.mult)
            t_hc = V([c_ha, c_is], v.tensor_tensor, hc0, hc0a, isl, A.add)
            for k in range(RD):
                t_nf = S([t_c16], s.activation, T["num%d" % k][:, 64:72], T.fl[:, ca:ca + 8], AF.Copy, scale=-0.0625)
            for k in range(1, RD):
                S([t_nil], s.activation, T["sat%d" % k][:, 0:1], nil, AF.Copy)
            for k in range(1, RD):
                t_a0 = S([t_xz], s.activation, T["at%d" % k][:, 256:512], T.xt[:, 256:512], AF.Copy)
        run("t", [t_z] + t_ua, te.matmul_mx, T.ha[:, 0:128], T.ua[:, :], T.uas[:, :], Zc[:, 0:128], Zs[:, 0:128], True, False)
        t_h = run("t", t_ub, te.matmul_mx, T.ha[:, 0:128], T.ub[:, :], T.ubs[:, :], Zc[:, 0:128], Zs[:, 0:128], False, True)
        want, cf = F(64), F(1)
        t_wn = V([t_h], v.tensor_scalar, want, T.ha[:, 0:64], 0.0, None, A.is_gt)
        t_sat = V([t_wn, t_c16], v.tensor_tensor_scan, sat[:, 1:65], want, c16, 0.0, A.add, A.min)
        cown = sat[:, 64:65]
        need("g", [t_sat])
        slots = {d: 7 - rank if rank > T.rank_of(d) else 6 - rank for d in side + [mate] + other}

        def give(ds, es):
            ds = [d for d in ds if wanted(rank, d, t)]
            if not ds:
                return []
            sent.append(len(es))
            sem = T.sem[("ac%d" if early(rank, ds[0]) else "ah%d") % t]
            return [RemoteDMATransfer(dst_ids=[did(d) for d in ds], dma_engine_mask=bits(es), remote_sem=sem, srcs=[cown],
                                      dsts=[land[:, slots[d]:slots[d] + 1] for d in ds])]

        ahead = urgent(rank, other[0])
        now = give(side + other if ahead else side, eoff) + give([mate], eon)
        tail = [] if ahead else give(other, eoff)
        if now:
            g.remote_dma_fused(now, local_sem=T.sem.loc)
        inc = {d: len(eon) if d == mate else len(eoff) for d in side + [mate] + other if wanted(T.rank_of(d), core, t)}
        soon = [d for d in inc if early(T.rank_of(d), core)]
        na, nac = len(soon), sum(inc[d] for d in soon)
        nah = sum(inc.values()) - nac
        hcx, stop, satm, encm, sgn, red = F(1), F(64), F(64), F(64), F(64), F(1)
        sa = at["fl"]
        seg, encw = F(64), T.fl[:, sa + 15:sa + 64:16]
        stopw, nine, wid, wj, tww, hdk, bcol = F(4), F(4), F(4), F(4), F(4), F(1), F(1)
        logo = O(1)
        t_rd = S([t_sat, c_kh], s.activation, sgn, sat[:, 1:65], AF.Sign, bias=kh, scale=-1.0, accum_out=red)
        t_cf.append(S([t_sat], s.activation, cf, cown, AF.Copy))
        counts.append(cf)
        if t:
            tot, hdn, hcn = F(1), F(1), F(1)
            t_to = V(late[t - 1], v.tensor_reduce, tot, T["cnt%d" % (t - 1)][:, 0:7], AxisListType.X, A.add)
        t_st = V([t_sat], v.tensor_tensor, stop, sat[:, 1:65], sat[:, 0:64], A.subtract)
        if t:
            t_hd = V([t_to, t_hd, t_cf[t - 1]], v.tensor_scalar, hdn, tot, counts[t - 1], hd, A.add, A.add)
        t_sm = V([c_m16], v.tensor_tensor, satm, sat[:, 1:65], m16, A.mult)
        if t:
            t_hc = V([t_hd], v.tensor_scalar, hcn, hdn, 0.125, hc0, A.mult, A.add)
            hd, hc = hdn, hcn
        t_hk = V([t_hd], v.tensor_scalar, hdk, hd, float(NR - 1), None, A.add)
        t_em = V([t_sm, t_st], v.tensor_tensor, encm, satm, stop, A.mult)
        t_hx = V([t_sat, c_sm, t_hc], v.tensor_scalar, hcx, cown, sm, hc, A.mult, A.add)
        for f in books[:2]:
            f()
        t_sg = V([t_em, c_rs], v.tensor_tensor_scan, seg, rst, encm, 0.0, A.mult, A.add)
        for f in books[2:4]:
            f()
        t_sw = V([t_sg], v.tensor_scalar, stopw, encw, 1.0, None, A.min)
        t_ni = V([t_sg], v.tensor_scalar, nine, encw, 9.0, None, A.is_ge)
        if t == 0:
            t_xp = [zeros("x1")]
            t_cz = zeros("cc")
            t_xp.append(zeros("x2"))
        pa = at["fl"]
        pre, pcol, lst = F(na), T.fl[:, pa + na - 1:pa + na], O(1)
        mask = T.fl[:, m7a + 7 - na:m7a + 7]
        P = BASE + QW * me
        ac = ("ac%d" % t, nac)
        late[t] = [ac] + ([("ah%d" % t, nah)] if nah else [])
        t_p = V([ac, c_m7], v.tensor_tensor_scan, pre, land[:, 7 - na:7], mask, 0.0, A.add, A.mult)
        t_ls = V([t_p, t_hx], v.tensor_scalar, lst, pcol, 0.125, hcx, A.mult, A.add)
        t_pc = V([t_ls, t_wq, ("pre", npre)], v.tensor_copy, Zc[:, P:P + 16].bitcast(u32), T.wq[:, :].bitcast(u32).indirect(lst))
        t_ps = S([t_ls, t_wq, ("pre", npre)], s.activation, Zs[:, P:P + 16], T.wqs[:, :].indirect(lst), AF.Copy)

        def codes(via):
            return [RemoteDMATransfer(dst_ids=[did(peers[e])], dma_engine_mask=bits(via[peers[e]]), remote_sem=T.sem["ak%d" % t],
                                      srcs=[Zc[:, P + 4 * e:P + 4 * e + 4].bitcast(u8)], dsts=[Zc[:, P:P + 4].bitcast(u8)])
                    for e in range(1, 4)]

        def scales(via, w):
            out = []
            for e in range(1, 4):
                o = 4 * e if w == 4 else 0
                out.append(RemoteDMATransfer(dst_ids=[did(peers[e])], dma_engine_mask=bits(via[peers[e]]), remote_sem=T.sem["ap%d" % t],
                                             srcs=[Zs[:, P + o:P + o + w]], dsts=[Zs[:, P + o - 4 * e:P + o - 4 * e + w]]))
            return out

        h = len(eon) // 2
        if t < RD - 1:
            need("g", [t_pc, t_ps])
            g.remote_dma_fused(codes({side[0]: eoff[:h], side[1]: eoff[h:2 * h], mate: eon[:h]}) +
                               scales({side[0]: eoff[2 * h:3 * h], side[1]: eoff[3 * h:], mate: eon[h:]}, 16), local_sem=T.sem.loc)
            ncol = 3 * h
        else:
            via = {side[0]: eoff[:2 * h], side[1]: eoff[2 * h:], mate: eon}
            need("g", [t_pc])
            g.remote_dma_fused(codes(via), local_sem=T.sem.loc)
            need("g", [t_ps])
            g.remote_dma_fused(scales(via, 4), local_sem=T.sem.loc)
            ncol = 6 * h
        sent.append(2 * ncol)
        if tail:
            g.remote_dma_fused(tail, local_sem=T.sem.loc)
        ends += [("ak%d" % t, ncol), ("ap%d" % t, ncol)] + late[t]
        vi, va, vx, vo = I(4), I(4), F(4), F(4)
        q = (F(64), F(64), F(64))
        pl = O(4)
        t_b = t_hk
        if rank:
            pr = F(1)
            t_pr = V([], v.tensor_reduce, pr, land[:, 7 - rank:7], AxisListType.X, A.add)
        t_wj = V([t_ni, c_jw], v.tensor_tensor, wj, nine, jw, A.add)
        t_lg = V([t_rd], v.tensor_scalar, logo, red, 0.5, 32.0, A.mult, A.add)
        if rank:
            t_b = V([t_hk, t_pr], v.tensor_tensor, bcol, hdk, pr, A.add)
        else:
            bcol = hdk
        t_wi = V([t_sw, c_jd], v.tensor_tensor, wid, stopw, jd, A.mult)
        t_vi = V([t_b, t_sg], v.tensor_scalar, vi, encw, bcol, float(2 ** SH + 1), A.add, A.mult)
        t_tw = V([t_wi, t_wj], v.tensor_tensor, tww, wid, wj, A.add)
        t_va = V([t_vi], v.tensor_scalar, va, vi, 1, 3 * QW + 2, A.logical_shift_right, A.bitwise_and)
        for f in books[4:5]:
            f()
        t_vx = V([t_va, t_sw], v.tensor_tensor, vx, va, stopw, A.mult)
        t_vo = V([t_vx, t_tw], v.tensor_tensor, vo, vx, tww, A.add)
        for f in books[5:]:
            f()
        t_pl = V([t_vo], v.tensor_copy, pl, vo)
        if t == 0:
            t_xp.append(zeros("x3"))
            t_vq = V([tv], v.quantize_mx, T.vq[:, :], T.vqs[:, :], T.vt[:, :])
        ra = 16 + 16 * t
        t_lks = S([t_lg, t_z, t_cz], s.activation, T.ccs[:, ra:ra + 16], Zs[:, 0:128].indirect(logo), AF.Copy)

        def book(bcol=bcol, t_b=t_b, q=q, t_lg=t_lg, t_z=t_z, t_st=t_st, stop=stop, sat=sat, num=num, numn=numn, ra=ra, logo=logo, Zc=Zc):
            k = {}

            def b0():
                t_lcs.append(V([t_lg, t_z, t_cz], v.tensor_copy, T.cc[:, ra:ra + 16].bitcast(u32), Zc[:, 0:128].bitcast(u32).indirect(logo)))

            def b1():
                k[1] = V([t_b], v.tensor_scalar, q[0], sat[:, 1:65], bcol, float(NR * PL - NR), A.add, A.add)

            def b2():
                t_lis.append(V(t_num + [t_fill, t_nf], v.tensor_copy, T.sidc[:, ra:ra + 16], num[:, 0:72].indirect(logo)))

            def b3():
                k[2] = V([k[1]] + t_num, v.tensor_tensor, q[1], q[0], num[:, 0:64], A.subtract)

            def b4():
                k[3] = V([k[2], t_st], v.tensor_tensor, q[2], q[1], stop, A.mult)

            def b5():
                t_num[:] = [V([k[3]], v.tensor_tensor, numn[:, 0:64], q[2], num[:, 0:64], A.add)]

            return [b0, b1, b2, b3, b4, b5]

        books = book()
        if t == RD - 2:
            d0, n2, d1, g1, g2, l1, l2 = F(1), F(1), F(1), F(3), F(3), F(3), F(3)
            lfin = O(3)
            e0 = V([t_cf[1]], v.tensor_scalar, d0, counts[0], -1.0, 16.0, A.mult, A.add)
            e1 = V([], v.tensor_tensor, n2, counts[0], counts[1], A.add)
            e2 = V([], v.tensor_scalar, d1, counts[1], -1.0, 16.0, A.mult, A.add)
            e4 = V([e0, c_jw], v.tensor_scalar, g1, jq, counts[0], d0, A.is_ge, A.mult)
            e5 = V([e1, e2], v.tensor_scalar, g2, jq, n2, d1, A.is_ge, A.mult)
            e6 = V([e4, c_j16], v.tensor_tensor, l1, g1, jq16, A.add)
            e7 = V([e5, e6], v.tensor_tensor, l2, l1, g2, A.add)
            t_lf = V([e7], v.tensor_copy, lfin, l2)
        if t == RD - 1:
            books[0]()
            t_l2 = S([t_lks, t_lf], s.activation, T.lgs[:, :], T.ccs[:, :].indirect(lfin), AF.Copy)
            t_l1 = V(t_lcs + [t_lf], v.tensor_copy, T.lg[:, :].bitcast(u32), T.cc[:, :].bitcast(u32).indirect(lfin))
            dma("y", [t_l1], "st", T.oc[:, 0:192], T.lg[:, :].bitcast(u8))
            for k in range(4):
                dma("y", [t_l2], "st", T.osc[4 * k:4 * k + 4, 0:48], T.lgs[32 * k:32 * k + 4, :])
        t_xc = V([t_pl, ("ak%d" % t, ncol), t_z, t_pc, t_xp[t]], v.tensor_copy, Nc[:, 0:64].bitcast(u32), Zc[:, :].bitcast(u32).indirect(pl))
        t_xs = S([t_pl, ("ap%d" % t, ncol), t_z, t_ps, t_xp[t]], s.activation, Ns[:, 0:64], Zs[:, :].indirect(pl), AF.Copy)
        t_X = [t_xc, t_xs]
    t_y = run("t", t_X + [t_vq], te.matmul_mx, T.py[:, 0:128], T.vq[:, :], T.vqs[:, :], T.x3[:, :], T.x3s[:, :], True, True)
    dma("y", [t_xc], "st", T.oc[:, 192:448], T.x3[:, 0:64].bitcast(u8))
    for k in range(4):
        dma("sy"[k % 2], [t_xs], "st", T.osc[4 * k:4 * k + 4, 48:112], T.x3s[32 * k:32 * k + 4, 0:64])
    t_yc = S([t_y], s.activation, T.ys[:, :], T.py[:, 0:64], AF.Copy)
    for f in books[1:4]:
        f()
    t_l3 = V(t_lis, v.tensor_copy, T.sidl[:, :], T.sidc[:, :].indirect(lfin))
    for f in books[4:]:
        f()
    dma("y", [t_l3], "st", T.sid[0:1, 0:48], T.sidl[0:1, :])
    dma("s", [t_yc], "st", T.y[:, :], T.ys[:, :])
    dma("y", t_num, "st", T.sid[0:1, 48:112], T["num%d" % RD][0:1, 0:64])
    need("g", list(done.items()) + list(dmas.items()) + [("loc", sum(sent)), ("pre", npre)] + ends)
